import numpy as np
import ml_dtypes


def mxq(x, axis, fmt="e4m3"):
    dtype, down = {"e4m3": (ml_dtypes.float8_e4m3fn, 7), "e5m2": (ml_dtypes.float8_e5m2, 14)}[fmt]
    v = np.moveaxis(np.asarray(x, np.float32).astype(ml_dtypes.bfloat16).astype(np.float64), axis, -1)
    blocks = v.reshape(v.shape[:-1] + (-1, 32))
    amax = np.abs(blocks).max(-1, keepdims=True)
    byte = np.maximum(np.where(amax > 0, np.frexp(amax)[1] - 1 + 127, 0) - down, 1)
    scale = np.exp2(byte - 127.0)
    codes = (blocks / scale).astype(np.float32).astype(dtype).astype(np.float64)
    return np.moveaxis((codes * scale).reshape(v.shape), -1, axis)


WIDE = False


def mx_kscale(k):
    if not WIDE:
        return np.ones(k)
    levels = np.array([30, -30])
    if k % 512:
        return np.exp2(np.random.permutation(np.resize(levels, k // 32))).repeat(32)
    a = np.empty((k // 512, 16))
    for p in range(k // 512):
        a[p, :8] = np.random.permutation(np.resize(levels, 8))
        for g in range(8):
            far = levels[np.abs(levels - a[p, g]) >= 10]
            a[p, g + 8] = far[np.random.randint(len(far))]
    return np.exp2(a.ravel()).repeat(32)


def f64(x):
    return np.asarray(x).astype(np.float64)


K, L, M, T = 1024, 1024, 512, 1536


def setup_inputs():
    n = np.random.standard_normal
    s1 = mx_kscale(K)[:, None]
    s2 = mx_kscale(L)[:, None]
    m = np.exp(0.5 * n((1, T)))
    return {
        "w": (n((K, M)) / np.sqrt(K) / s1).astype(np.float32),
        "dy": (m * n((K, T)) * s1).astype(np.float32),
        "v": (n((L, M)) / np.sqrt(L) / s2).astype(np.float32),
        "e": (n((L, T)) * s2).astype(np.float32),
    }


def reference(w, dy, v, e):
    w_ = mxq(f64(w), 0, "e4m3")
    dy_ = mxq(f64(dy), 0, "e5m2")
    v_ = mxq(f64(v), 0, "e4m3")
    e_ = mxq(f64(e), 0, "e4m3")
    y = w_.T @ dy_ + v_.T @ e_
    return y

@@ -1,0 +1,150 @@
+from contextlib import ExitStack
+
+import concourse.mybir as mybir
+
+K, L, M, T = 1024, 1024, 512, 1536
+FLOPS = 2 * (K + L) * M * T
+
+F32 = mybir.dt.float32
+BF16 = mybir.dt.bfloat16
+U32 = mybir.dt.uint32
+U8 = mybir.dt.uint8
+E4M3 = mybir.dt.float8_e4m3fn_x4
+E5M2 = mybir.dt.float8_e5m2_x4
+
+P = 128
+J = 4
+K_PASS = P * J
+CHUNK = 512
+HALF = 256
+V_COLS = 144
+
+
+def tile_mix_aux_fm_none_kernel(tc, w, dy, v, e, out):
+    nc = tc.nc
+    hbm = {"w": w, "dy": dy, "v": v, "e": e}
+    fmt = {"w": E4M3, "dy": E5M2, "v": E4M3, "e": E4M3}
+    loads = [
+        ("w", 0, 0, 512),
+        ("dy", 0, 0, 1536),
+        ("e", 0, 0, 1024),
+        ("v", 0, 0, 512),
+        ("e", 1, 0, 1024),
+        ("v", 1, 0, 512),
+        ("w", 1, 0, 512),
+        ("dy", 1, 512, 512),
+        ("dy", 1, 0, 512),
+        ("e", 1, 1024, 512),
+        ("e", 0, 1024, 512),
+        ("dy", 1, 1024, 512),
+    ]
+
+    with ExitStack() as ctx:
+        keep = ctx.enter_context(tc.tile_pool(name="keep", bufs=1))
+        stage = ctx.enter_context(tc.tile_pool(name="stage", bufs=6))
+        psum = ctx.enter_context(tc.psum_pool(name="psum", bufs=2))
+        ctx.enter_context(tc.manual_schedule())
+
+        raw = {}
+        for name, g, c0, cols in loads:
+            t = keep.tile([P, J, cols], F32, name="raw_%s%d_%d" % (name, g, c0))
+            nc.sync.dma_start(
+                out=t[:],
+                in_=hbm[name][g * K_PASS : (g + 1) * K_PASS, c0 : c0 + cols].rearrange("(p j) c -> p j c", j=J),
+            )
+            raw[name, g, c0] = t
+
+        codes, scales = {}, {}
+        for name in ("w", "dy", "v", "e"):
+            width = hbm[name].shape[1]
+            codes[name] = keep.tile([P, 2, width], U32, name="codes_" + name, align_bytes=64)
+            scales[name] = keep.tile([P, 2, width], U8, name="scales_" + name, align_bytes=64)
+
+        def interleave(name, g, c0, h, v_cols):
+            b = stage.tile([P, HALF, J], BF16, name="grouped", align_bytes=64)
+            for copy, lo, hi in ((nc.vector.tensor_copy, 0, v_cols), (nc.scalar.copy, v_cols, HALF)):
+                copy(
+                    out=b[:, lo:hi, :].rearrange("p (c i) j -> p c j i", i=4),
+                    in_=raw[name, g, c0][:, :, h + lo : h + hi].rearrange("p j (c i) -> p c j i", i=4),
+                )
+            return b
+
+        def quantise(name, g, c0, h, b):
+            cols = slice(c0 + h, c0 + h + HALF)
+            nc.vector.quantize_mx(
+                out=codes[name][:, g, cols].bitcast(fmt[name]),
+                scales=scales[name][:, g, cols],
+                in_=b[:].rearrange("p c j -> p (c j)"),
+            )
+
+        def prep(name, g, c0, v_cols=V_COLS):
+            width = raw[name, g, c0].shape[2]
+            last = None
+            for h in range(0, width, HALF):
+                b = interleave(name, g, c0, h, v_cols)
+                if last is not None:
+                    quantise(name, g, c0, h - HALF, last)
+                last = b
+            quantise(name, g, c0, width - HALF, last)
+
+        acc = {}
+
+        def passes(c, sta, mov, g, start=False, stop=False, n0=0, n=CHUNK):
+            for m in range(M // P):
+                if start:
+                    acc[c, m] = psum.tile([P, CHUNK], F32, name="acc%d" % m)
+                rows = slice(m * P, (m + 1) * P)
+                cols = slice(c * CHUNK + n0, c * CHUNK + n0 + n)
+                nc.tensor.matmul_mx(
+                    out=acc[c, m][:, n0 : n0 + n],
+                    lhsT=codes[sta][:, g, rows].bitcast(fmt[sta]),
+                    lhsT_scale=scales[sta][:, g, rows],
+                    rhs=codes[mov][:, g, cols].bitcast(fmt[mov]),
+                    rhs_scale=scales[mov][:, g, cols],
+                    start=start,
+                    stop=stop,
+                )
+
+        res = [keep.tile([P, M // P, CHUNK], F32, name="res%d" % c) for c in range(3)]
+
+        def drain(c):
+            for m in range(M // P):
+                copy = nc.vector.tensor_copy if m % 2 else nc.scalar.copy
+                copy(out=res[c][:, m, :], in_=acc[c, m][:])
+
+        def store(c, m0, m1):
+            rows = out[m0 * P : m1 * P, c * CHUNK : (c + 1) * CHUNK]
+            nc.sync.dma_start(out=rows.rearrange("(m p) t -> p m t", p=P), in_=res[c][:, m0:m1, :])
+
+        prep("w", 0, 0)
+        prep("dy", 0, 0)
+        passes(0, "w", "dy", 0, start=True)
+        passes(1, "w", "dy", 0, start=True)
+        prep("e", 0, 0)
+        prep("v", 0, 0)
+        passes(0, "v", "e", 0)
+        passes(1, "v", "e", 0)
+        prep("e", 1, 0)
+        prep("v", 1, 0)
+        passes(0, "v", "e", 1)
+        passes(1, "v", "e", 1)
+        prep("w", 1, 0)
+        prep("dy", 1, 512)
+        passes(1, "w", "dy", 1, stop=True)
+        prep("dy", 1, 0)
+        passes(0, "w", "dy", 1, stop=True)
+        drain(1)
+        store(1, 0, 4)
+        passes(2, "w", "dy", 0, start=True)
+        prep("e", 1, 1024)
+        passes(2, "v", "e", 1)
+        drain(0)
+        store(0, 0, 4)
+        prep("e", 0, 1024)
+        passes(2, "v", "e", 0)
+        prep("dy", 1, 1024, 168)
+        passes(2, "w", "dy", 1, stop=True)
+        drain(2)
+        store(2, 0, 1)
+        store(2, 1, 2)
+        store(2, 2, 4)

@@ -16,8 +16,8 @@ P = 128
 J = 4
 K_PASS = P * J
 CHUNK = 512
-HALF = 256
-V_COLS = 144
+VW = 240
+VH = 128
 
 
 def tile_mix_aux_fm_none_kernel(tc, w, dy, v, e, out):
@@ -25,23 +25,21 @@ def tile_mix_aux_fm_none_kernel(tc, w, dy, v, e, out):
     hbm = {"w": w, "dy": dy, "v": v, "e": e}
     fmt = {"w": E4M3, "dy": E5M2, "v": E4M3, "e": E4M3}
     loads = [
-        ("w", 0, 0, 512),
         ("dy", 0, 0, 1536),
-        ("e", 0, 0, 1024),
+        ("w", 0, 0, 512),
+        ("e", 0, 0, 1536),
+        ("dy", 1, 0, 1536),
         ("v", 0, 0, 512),
-        ("e", 1, 0, 1024),
-        ("v", 1, 0, 512),
         ("w", 1, 0, 512),
-        ("dy", 1, 512, 512),
-        ("dy", 1, 0, 512),
+        ("e", 1, 0, 512),
+        ("v", 1, 0, 512),
+        ("e", 1, 512, 512),
         ("e", 1, 1024, 512),
-        ("e", 0, 1024, 512),
-        ("dy", 1, 1024, 512),
     ]
 
     with ExitStack() as ctx:
         keep = ctx.enter_context(tc.tile_pool(name="keep", bufs=1))
-        stage = ctx.enter_context(tc.tile_pool(name="stage", bufs=6))
+        stage = ctx.enter_context(tc.tile_pool(name="stage", bufs=5))
         psum = ctx.enter_context(tc.psum_pool(name="psum", bufs=2))
         ctx.enter_context(tc.manual_schedule())
 
@@ -52,99 +50,118 @@ def tile_mix_aux_fm_none_kernel(tc, w, dy, v, e, out):
                 out=t[:],
                 in_=hbm[name][g * K_PASS : (g + 1) * K_PASS, c0 : c0 + cols].rearrange("(p j) c -> p j c", j=J),
             )
-            raw[name, g, c0] = t
+            for c in range(0, cols, P):
+                raw[name, g, c0 + c] = (t, c)
 
         codes, scales = {}, {}
         for name in ("w", "dy", "v", "e"):
             width = hbm[name].shape[1]
-            codes[name] = keep.tile([P, 2, width], U32, name="codes_" + name, align_bytes=64)
-            scales[name] = keep.tile([P, 2, width], U8, name="scales_" + name, align_bytes=64)
+            for g in range(2):
+                codes[name, g] = keep.tile([P, width], U32, name="codes_%s%d" % (name, g), align_bytes=64)
+                scales[name, g] = keep.tile([P, width], U8, name="scales_%s%d" % (name, g), align_bytes=64)
 
-        def interleave(name, g, c0, h, v_cols):
-            b = stage.tile([P, HALF, J], BF16, name="grouped", align_bytes=64)
-            for copy, lo, hi in ((nc.vector.tensor_copy, 0, v_cols), (nc.scalar.copy, v_cols, HALF)):
-                copy(
-                    out=b[:, lo:hi, :].rearrange("p (c i) j -> p c j i", i=4),
-                    in_=raw[name, g, c0][:, :, h + lo : h + hi].rearrange("p j (c i) -> p c j i", i=4),
-                )
-            return b
+        def interleave(name, g, c0, cols, v_cols):
+            b = stage.tile([P, cols, J], BF16, name="grouped", align_bytes=64)
+            t, h = raw[name, g, c0]
+            for copy, lo, hi in ((nc.vector.tensor_copy, 0, v_cols), (nc.scalar.copy, v_cols, cols)):
+                if hi > lo:
+                    copy(
+                        out=b[:, lo:hi, :].rearrange("p (c i) j -> p c j i", i=4),
+                        in_=t[:, :, h + lo : h + hi].rearrange("p j (c i) -> p c j i", i=4),
+                    )
+            return (name, g, c0, cols, b)
 
-        def quantise(name, g, c0, h, b):
-            cols = slice(c0 + h, c0 + h + HALF)
+        def quantise(job):
+            name, g, c0, cols, b = job
             nc.vector.quantize_mx(
-                out=codes[name][:, g, cols].bitcast(fmt[name]),
-                scales=scales[name][:, g, cols],
+                out=codes[name, g][:, c0 : c0 + cols].bitcast(fmt[name]),
+                scales=scales[name, g][:, c0 : c0 + cols],
                 in_=b[:].rearrange("p c j -> p (c j)"),
             )
 
-        def prep(name, g, c0, v_cols=V_COLS):
-            width = raw[name, g, c0].shape[2]
+        def prep(parts):
             last = None
-            for h in range(0, width, HALF):
-                b = interleave(name, g, c0, h, v_cols)
+            for part in parts:
+                job = interleave(*part)
                 if last is not None:
-                    quantise(name, g, c0, h - HALF, last)
-                last = b
-            quantise(name, g, c0, width - HALF, last)
+                    quantise(last)
+                last = job
+            quantise(last)
 
         acc = {}
 
-        def passes(c, sta, mov, g, start=False, stop=False, n0=0, n=CHUNK):
-            for m in range(M // P):
-                if start:
-                    acc[c, m] = psum.tile([P, CHUNK], F32, name="acc%d" % m)
-                rows = slice(m * P, (m + 1) * P)
-                cols = slice(c * CHUNK + n0, c * CHUNK + n0 + n)
-                nc.tensor.matmul_mx(
-                    out=acc[c, m][:, n0 : n0 + n],
-                    lhsT=codes[sta][:, g, rows].bitcast(fmt[sta]),
-                    lhsT_scale=scales[sta][:, g, rows],
-                    rhs=codes[mov][:, g, cols].bitcast(fmt[mov]),
-                    rhs_scale=scales[mov][:, g, cols],
-                    start=start,
-                    stop=stop,
-                )
+        def one_pass(c, m, sta, mov, g, start=False, stop=False, n0=0, n=CHUNK):
+            if start:
+                acc[c, m] = psum.tile([P, CHUNK], F32, name="acc%d" % m)
+            rows = slice(m * P, (m + 1) * P)
+            cols = slice(c * CHUNK + n0, c * CHUNK + n0 + n)
+            nc.tensor.matmul_mx(
+                out=acc[c, m][:, n0 : n0 + n],
+                lhsT=codes[sta, g][:, rows].bitcast(fmt[sta]),
+                lhsT_scale=scales[sta, g][:, rows],
+                rhs=codes[mov, g][:, cols].bitcast(fmt[mov]),
+                rhs_scale=scales[mov, g][:, cols],
+                start=start,
+                stop=stop,
+            )
 
-        res = [keep.tile([P, M // P, CHUNK], F32, name="res%d" % c) for c in range(3)]
+        def passes(c, sta, mov, g, ms=range(M // P), **kw):
+            for m in ms:
+                one_pass(c, m, sta, mov, g, **kw)
 
-        def drain(c):
-            for m in range(M // P):
-                copy = nc.vector.tensor_copy if m % 2 else nc.scalar.copy
-                copy(out=res[c][:, m, :], in_=acc[c, m][:])
+        res = [keep.tile([P, M // P, CHUNK], F32, name="res%d" % c) for c in range(T // CHUNK)]
 
-        def store(c, m0, m1):
-            rows = out[m0 * P : m1 * P, c * CHUNK : (c + 1) * CHUNK]
-            nc.sync.dma_start(out=rows.rearrange("(m p) t -> p m t", p=P), in_=res[c][:, m0:m1, :])
+        def drain(c, m, eng):
+            copy = nc.vector.tensor_copy if eng == "v" else nc.scalar.copy
+            copy(out=res[c][:, m, :], in_=acc[c, m][:])
 
-        prep("w", 0, 0)
-        prep("dy", 0, 0)
+        def store(c0, c1, m0, m1):
+            rows = out[m0 * P : m1 * P, c0 * CHUNK : c1 * CHUNK]
+            nc.sync.dma_start(
+                out=rows.rearrange("(m p) t -> p m t", p=P), in_=res[c0][:, m0:m1, :]
+            )
+
+        prep([("dy", 0, c, 512, VW) for c in (0, 512, 1024)] + [("w", 0, 0, 512, VW)])
         passes(0, "w", "dy", 0, start=True)
         passes(1, "w", "dy", 0, start=True)
-        prep("e", 0, 0)
-        prep("v", 0, 0)
+        prep([("e", 0, c, 512, VW) for c in (0, 512, 1024)])
+        prep([("dy", 1, 0, 512, VW), ("dy", 1, 512, 512, VW), ("v", 0, 0, 512, VW),
+              ("dy", 1, 1024, 512, VW), ("w", 1, 0, 256, VH), ("w", 1, 256, 256, VH)])
         passes(0, "v", "e", 0)
         passes(1, "v", "e", 0)
-        prep("e", 1, 0)
-        prep("v", 1, 0)
-        passes(0, "v", "e", 1)
-        passes(1, "v", "e", 1)
-        prep("w", 1, 0)
-        prep("dy", 1, 512)
-        passes(1, "w", "dy", 1, stop=True)
-        prep("dy", 1, 0)
-        passes(0, "w", "dy", 1, stop=True)
-        drain(1)
-        store(1, 0, 4)
-        passes(2, "w", "dy", 0, start=True)
-        prep("e", 1, 1024)
-        passes(2, "v", "e", 1)
-        drain(0)
-        store(0, 0, 4)
-        prep("e", 0, 1024)
-        passes(2, "v", "e", 0)
-        prep("dy", 1, 1024, 168)
-        passes(2, "w", "dy", 1, stop=True)
-        drain(2)
-        store(2, 0, 1)
-        store(2, 1, 2)
-        store(2, 2, 4)
+        passes(0, "w", "dy", 1)
+        passes(1, "w", "dy", 1)
+        prep([("e", 1, 0, 256, VH), ("e", 1, 256, 256, VH)])
+        prep([("v", 1, 0, 256, 160), ("v", 1, 256, 256, 128)])
+        passes(0, "v", "e", 1, stop=True)
+        def early(m):
+            one_pass(2, m, "w", "dy", 0, start=True)
+            one_pass(2, m, "v", "e", 0)
+            one_pass(2, m, "w", "dy", 1)
+        drain(0, 0, "s")
+        drain(0, 1, "v")
+        store(0, 1, 0, 2)
+        drain(0, 2, "s")
+        early(0)
+        early(1)
+        prep([("e", 1, 512, 256, 192), ("e", 1, 768, 256, 160)])
+        drain(0, 3, "s")
+        store(0, 1, 2, 4)
+        passes(1, "v", "e", 1, stop=True)
+        early(2)
+        early(3)
+        drain(1, 0, "s")
+        store(1, 2, 0, 1)
+        drain(1, 1, "s")
+        store(1, 2, 1, 2)
+        drain(1, 2, "s")
+        drain(1, 3, "s")
+        store(1, 2, 2, 4)
+        prep([("e", 1, 1024, 256, 256), ("e", 1, 1280, 256, 256)])
+        passes(2, "v", "e", 1, stop=True)
+        drain(2, 0, "s")
+        drain(2, 1, "v")
+        store(2, 3, 0, 2)
+        drain(2, 2, "s")
+        drain(2, 3, "v")
+        store(2, 3, 2, 4)

@@ -18,6 +18,8 @@ K_PASS = P * J
 CHUNK = 512
 VW = 240
 VH = 128
+VT = 184
+VL = 152
 
 
 def tile_mix_aux_fm_none_kernel(tc, w, dy, v, e, out):
@@ -28,12 +30,13 @@ def tile_mix_aux_fm_none_kernel(tc, w, dy, v, e, out):
         ("dy", 0, 0, 1536),
         ("w", 0, 0, 512),
         ("e", 0, 0, 1536),
-        ("dy", 1, 0, 1536),
+        ("dy", 1, 0, 1024),
         ("v", 0, 0, 512),
         ("w", 1, 0, 512),
         ("e", 1, 0, 512),
         ("v", 1, 0, 512),
         ("e", 1, 512, 512),
+        ("dy", 1, 1024, 512),
         ("e", 1, 1024, 512),
     ]
 
@@ -109,59 +112,59 @@ def tile_mix_aux_fm_none_kernel(tc, w, dy, v, e, out):
             for m in ms:
                 one_pass(c, m, sta, mov, g, **kw)
 
-        res = [keep.tile([P, M // P, CHUNK], F32, name="res%d" % c) for c in range(T // CHUNK)]
+        res = [keep.tile([P, M // P, T], F32, name="res")]
 
         def drain(c, m, eng):
             copy = nc.vector.tensor_copy if eng == "v" else nc.scalar.copy
-            copy(out=res[c][:, m, :], in_=acc[c, m][:])
+            copy(out=res[0][:, m, c * CHUNK : (c + 1) * CHUNK], in_=acc[c, m][:])
 
         def store(c0, c1, m0, m1):
             rows = out[m0 * P : m1 * P, c0 * CHUNK : c1 * CHUNK]
             nc.sync.dma_start(
-                out=rows.rearrange("(m p) t -> p m t", p=P), in_=res[c0][:, m0:m1, :]
+                out=rows.rearrange("(m p) t -> p m t", p=P), in_=res[0][:, m0:m1, c0 * CHUNK : c1 * CHUNK]
             )
 
         prep([("dy", 0, c, 512, VW) for c in (0, 512, 1024)] + [("w", 0, 0, 512, VW)])
         passes(0, "w", "dy", 0, start=True)
         passes(1, "w", "dy", 0, start=True)
         prep([("e", 0, c, 512, VW) for c in (0, 512, 1024)])
-        prep([("dy", 1, 0, 512, VW), ("dy", 1, 512, 512, VW), ("v", 0, 0, 512, VW),
-              ("dy", 1, 1024, 512, VW), ("w", 1, 0, 256, VH), ("w", 1, 256, 256, VH)])
+        prep([("dy", 1, 0, 512, VW), ("dy", 1, 512, 512, VW), ("v", 0, 0, 256, VH), ("v", 0, 256, 256, VH)])
         passes(0, "v", "e", 0)
         passes(1, "v", "e", 0)
+        prep([("w", 1, 0, 256, VH), ("w", 1, 256, 256, VH)])
         passes(0, "w", "dy", 1)
         passes(1, "w", "dy", 1)
         prep([("e", 1, 0, 256, VH), ("e", 1, 256, 256, VH)])
-        prep([("v", 1, 0, 256, 160), ("v", 1, 256, 256, 128)])
+        prep([("v", 1, 0, 256, VH), ("v", 1, 256, 256, VH)])
         passes(0, "v", "e", 1, stop=True)
+        drain(0, 0, "s")
+        drain(0, 1, "v")
+        drain(0, 2, "s")
         def early(m):
             one_pass(2, m, "w", "dy", 0, start=True)
             one_pass(2, m, "v", "e", 0)
-            one_pass(2, m, "w", "dy", 1)
-        drain(0, 0, "s")
-        drain(0, 1, "v")
-        store(0, 1, 0, 2)
-        drain(0, 2, "s")
         early(0)
         early(1)
-        prep([("e", 1, 512, 256, 192), ("e", 1, 768, 256, 160)])
+        prep([("e", 1, 512, 256, 160), ("e", 1, 768, 256, 160)])
         drain(0, 3, "s")
-        store(0, 1, 2, 4)
-        passes(1, "v", "e", 1, stop=True)
+        passes(1, "v", "e", 1, n0=0, n=256)
+        passes(1, "v", "e", 1, n0=256, n=256, stop=True)
         early(2)
         early(3)
         drain(1, 0, "s")
-        store(1, 2, 0, 1)
-        drain(1, 1, "s")
-        store(1, 2, 1, 2)
+        store(0, 2, 0, 1)
+        drain(1, 1, "v")
+        store(0, 2, 1, 2)
+        prep([("dy", 1, 1024, 256, VT), ("dy", 1, 1280, 256, VT)])
         drain(1, 2, "s")
+        store(0, 2, 2, 3)
         drain(1, 3, "s")
-        store(1, 2, 2, 4)
-        prep([("e", 1, 1024, 256, 256), ("e", 1, 1280, 256, 256)])
-        passes(2, "v", "e", 1, stop=True)
-        drain(2, 0, "s")
-        drain(2, 1, "v")
-        store(2, 3, 0, 2)
-        drain(2, 2, "s")
-        drain(2, 3, "v")
-        store(2, 3, 2, 4)
+        store(0, 2, 3, 4)
+        passes(2, "w", "dy", 1)
+        prep([("e", 1, 1024, 256, VL), ("e", 1, 1280, 256, VL)])
+        passes(2, "v", "e", 1, ms=(0, 1), n0=0, n=256)
+        passes(2, "v", "e", 1, ms=(0, 1), n0=256, n=256, stop=True)
+        passes(2, "v", "e", 1, ms=(2, 3), stop=True)
+        for m in range(4):
+            drain(2, m, "sv"[m % 2])
+            store(2, 3, m, m + 1)

@@ -17,7 +17,7 @@ J = 4
 K_PASS = P * J
 CHUNK = 512
 VW = 240
-VH = 128
+VH = 136
 VT = 184
 VL = 152
 
@@ -114,14 +114,14 @@ def tile_mix_aux_fm_none_kernel(tc, w, dy, v, e, out):
 
         res = [keep.tile([P, M // P, T], F32, name="res")]
 
-        def drain(c, m, eng):
+        def drain(c, m, eng, n0=0, n=CHUNK):
             copy = nc.vector.tensor_copy if eng == "v" else nc.scalar.copy
-            copy(out=res[0][:, m, c * CHUNK : (c + 1) * CHUNK], in_=acc[c, m][:])
+            copy(out=res[0][:, m, c * CHUNK + n0 : c * CHUNK + n0 + n], in_=acc[c, m][:, n0 : n0 + n])
 
-        def store(c0, c1, m0, m1):
-            rows = out[m0 * P : m1 * P, c0 * CHUNK : c1 * CHUNK]
+        def store(t0, t1, m0, m1):
+            rows = out[m0 * P : m1 * P, t0:t1]
             nc.sync.dma_start(
-                out=rows.rearrange("(m p) t -> p m t", p=P), in_=res[0][:, m0:m1, c0 * CHUNK : c1 * CHUNK]
+                out=rows.rearrange("(m p) t -> p m t", p=P), in_=res[0][:, m0:m1, t0:t1]
             )
 
         prep([("dy", 0, c, 512, VW) for c in (0, 512, 1024)] + [("w", 0, 0, 512, VW)])
@@ -139,32 +139,41 @@ def tile_mix_aux_fm_none_kernel(tc, w, dy, v, e, out):
         passes(0, "v", "e", 1, stop=True)
         drain(0, 0, "s")
         drain(0, 1, "v")
-        drain(0, 2, "s")
         def early(m):
             one_pass(2, m, "w", "dy", 0, start=True)
             one_pass(2, m, "v", "e", 0)
+        store(0, 512, 0, 1)
         early(0)
         early(1)
-        prep([("e", 1, 512, 256, 160), ("e", 1, 768, 256, 160)])
-        drain(0, 3, "s")
-        passes(1, "v", "e", 1, n0=0, n=256)
-        passes(1, "v", "e", 1, n0=256, n=256, stop=True)
+        prep([("e", 1, 512, 256, VL), ("e", 1, 768, 256, VL)])
+        passes(1, "v", "e", 1, ms=(0, 1), n0=0, n=256)
+        passes(1, "v", "e", 1, ms=(0, 1), n0=256, n=256, stop=True)
+        passes(1, "v", "e", 1, ms=(2, 3), stop=True)
+        drain(0, 2, "s")
+        drain(0, 3, "v")
         early(2)
         early(3)
         drain(1, 0, "s")
-        store(0, 2, 0, 1)
+        store(512, 1024, 0, 1)
         drain(1, 1, "v")
-        store(0, 2, 1, 2)
+        store(0, 1024, 1, 2)
         prep([("dy", 1, 1024, 256, VT), ("dy", 1, 1280, 256, VT)])
         drain(1, 2, "s")
-        store(0, 2, 2, 3)
+        store(0, 1024, 2, 3)
         drain(1, 3, "s")
-        store(0, 2, 3, 4)
+        store(0, 1024, 3, 4)
         passes(2, "w", "dy", 1)
         prep([("e", 1, 1024, 256, VL), ("e", 1, 1280, 256, VL)])
         passes(2, "v", "e", 1, ms=(0, 1), n0=0, n=256)
         passes(2, "v", "e", 1, ms=(0, 1), n0=256, n=256, stop=True)
         passes(2, "v", "e", 1, ms=(2, 3), stop=True)
-        for m in range(4):
-            drain(2, m, "sv"[m % 2])
-            store(2, 3, m, m + 1)
+        drain(2, 0, "s", 0, 256)
+        store(1024, 1280, 0, 1)
+        drain(2, 1, "v")
+        store(1024, 1536, 1, 2)
+        drain(2, 0, "s", 256, 256)
+        store(1280, 1536, 0, 1)
+        drain(2, 2, "s")
+        store(1024, 1536, 2, 3)
+        drain(2, 3, "v")
+        store(1024, 1536, 3, 4)

@@ -69,8 +69,8 @@ def tile_mix_aux_fm_none_kernel(tc, w, dy, v, e, out):
             for copy, lo, hi in ((nc.vector.tensor_copy, 0, v_cols), (nc.scalar.copy, v_cols, cols)):
                 if hi > lo:
                     copy(
-                        out=b[:, lo:hi, :].rearrange("p (c i) j -> p c j i", i=4),
-                        in_=t[:, :, h + lo : h + hi].rearrange("p j (c i) -> p c j i", i=4),
+                        out=b[:, lo:hi, :].rearrange("p (c i) j -> p c j i", i=2),
+                        in_=t[:, :, h + lo : h + hi].rearrange("p j (c i) -> p c j i", i=2),
                     )
             return (name, g, c0, cols, b)
 

@@ -16,10 +16,15 @@ P = 128
 J = 4
 K_PASS = P * J
 CHUNK = 512
-VW = 240
-VH = 136
-VT = 184
-VL = 152
+VW = 248
+VH = 128
+VQ = 80
+VL = 96
+CUT = 896
+
+
+def bank(c, m):
+    return m if c in (0, 3) else 4 + m
 
 
 def tile_mix_aux_fm_none_kernel(tc, w, dy, v, e, out):
@@ -27,23 +32,21 @@ def tile_mix_aux_fm_none_kernel(tc, w, dy, v, e, out):
     hbm = {"w": w, "dy": dy, "v": v, "e": e}
     fmt = {"w": E4M3, "dy": E5M2, "v": E4M3, "e": E4M3}
     loads = [
-        ("dy", 0, 0, 1536),
         ("w", 0, 0, 512),
-        ("e", 0, 0, 1536),
-        ("dy", 1, 0, 1024),
-        ("v", 0, 0, 512),
         ("w", 1, 0, 512),
-        ("e", 1, 0, 512),
+        ("dy", 0, 0, 1536),
+        ("dy", 1, 0, 1536),
+        ("e", 0, 0, 1536),
+        ("e", 1, 0, 896),
+        ("v", 0, 0, 512),
         ("v", 1, 0, 512),
-        ("e", 1, 512, 512),
-        ("dy", 1, 1024, 512),
-        ("e", 1, 1024, 512),
+        ("e", 1, 896, 640),
     ]
 
     with ExitStack() as ctx:
         keep = ctx.enter_context(tc.tile_pool(name="keep", bufs=1))
-        stage = ctx.enter_context(tc.tile_pool(name="stage", bufs=5))
-        psum = ctx.enter_context(tc.psum_pool(name="psum", bufs=2))
+        stage = ctx.enter_context(tc.tile_pool(name="stage", bufs=6))
+        psum = ctx.enter_context(tc.psum_pool(name="psum", bufs=1))
         ctx.enter_context(tc.manual_schedule())
 
         raw = {}
@@ -93,9 +96,9 @@ def tile_mix_aux_fm_none_kernel(tc, w, dy, v, e, out):
 
         acc = {}
 
-        def one_pass(c, m, sta, mov, g, start=False, stop=False, n0=0, n=CHUNK):
+        def one_pass(c, m, sta, mov, g, start=False, stop=False, n0=0, n=CHUNK, fresh=None):
             if start:
-                acc[c, m] = psum.tile([P, CHUNK], F32, name="acc%d" % m)
+                acc[c, m] = psum.tile([P, CHUNK], F32, name="bank%d" % bank(c if fresh is None else fresh, m))
             rows = slice(m * P, (m + 1) * P)
             cols = slice(c * CHUNK + n0, c * CHUNK + n0 + n)
             nc.tensor.matmul_mx(
@@ -124,56 +127,97 @@ def tile_mix_aux_fm_none_kernel(tc, w, dy, v, e, out):
                 out=rows.rearrange("(m p) t -> p m t", p=P), in_=res[0][:, m0:m1, t0:t1]
             )
 
-        prep([("dy", 0, c, 512, VW) for c in (0, 512, 1024)] + [("w", 0, 0, 512, VW)])
+        def close(m):
+            one_pass(0, m, "v", "e", 1, stop=True)
+            one_pass(1, m, "v", "e", 1, n0=0, n=256)
+            one_pass(1, m, "v", "e", 1, n0=256, n=128, stop=True)
+
+        def both(m):
+            for c in (0, 1):
+                one_pass(c, m, "v", "e", 0)
+
+        def add(key, m, t0, n):
+            part = res[0][:, m, t0 : t0 + n]
+            nc.vector.tensor_tensor(out=part, in0=late[key, m][:, 0:n], in1=part, op=mybir.AluOpType.add)
+
+        late = {}
+
+        def late_pass(key, m, b, g, t0, n, start, stop, at=0):
+            if start:
+                late[key, m] = psum.tile([P, CHUNK], F32, name="bank%d" % b)
+            rows = slice(m * P, (m + 1) * P)
+            cols = slice(t0, t0 + n)
+            nc.tensor.matmul_mx(
+                out=late[key, m][:, at : at + n],
+                lhsT=codes["v", g][:, rows].bitcast(E4M3),
+                lhsT_scale=scales["v", g][:, rows],
+                rhs=codes["e", g][:, cols].bitcast(E4M3),
+                rhs_scale=scales["e", g][:, cols],
+                start=start,
+                stop=stop,
+            )
+
+        prep([("w", 0, 0, 512, VW), ("w", 1, 0, 512, VW)])
+        prep([("dy", 0, c, 512, VW) for c in (0, 1024, 512)])
         passes(0, "w", "dy", 0, start=True)
-        passes(1, "w", "dy", 0, start=True)
-        prep([("e", 0, c, 512, VW) for c in (0, 512, 1024)])
-        prep([("dy", 1, 0, 512, VW), ("dy", 1, 512, 512, VW), ("v", 0, 0, 256, VH), ("v", 0, 256, 256, VH)])
-        passes(0, "v", "e", 0)
-        passes(1, "v", "e", 0)
-        prep([("w", 1, 0, 256, VH), ("w", 1, 256, 256, VH)])
+        passes(2, "w", "dy", 0, ms=(0, 1, 2), start=True)
+        prep([("dy", 1, c, 512, VW) for c in (1024, 0, 512)])
+        passes(2, "w", "dy", 1, ms=(0, 1, 2), stop=True)
         passes(0, "w", "dy", 1)
-        passes(1, "w", "dy", 1)
-        prep([("e", 1, 0, 256, VH), ("e", 1, 256, 256, VH)])
-        prep([("v", 1, 0, 256, VH), ("v", 1, 256, 256, VH)])
-        passes(0, "v", "e", 1, stop=True)
-        drain(0, 0, "s")
-        drain(0, 1, "v")
-        def early(m):
-            one_pass(2, m, "w", "dy", 0, start=True)
-            one_pass(2, m, "v", "e", 0)
-        store(0, 512, 0, 1)
-        early(0)
-        early(1)
-        prep([("e", 1, 512, 256, VL), ("e", 1, 768, 256, VL)])
-        passes(1, "v", "e", 1, ms=(0, 1), n0=0, n=256)
-        passes(1, "v", "e", 1, ms=(0, 1), n0=256, n=256, stop=True)
-        passes(1, "v", "e", 1, ms=(2, 3), stop=True)
-        drain(0, 2, "s")
-        drain(0, 3, "v")
-        early(2)
-        early(3)
-        drain(1, 0, "s")
-        store(512, 1024, 0, 1)
-        drain(1, 1, "v")
-        store(0, 1024, 1, 2)
-        prep([("dy", 1, 1024, 256, VT), ("dy", 1, 1280, 256, VT)])
-        drain(1, 2, "s")
-        store(0, 1024, 2, 3)
-        drain(1, 3, "s")
-        store(0, 1024, 3, 4)
-        passes(2, "w", "dy", 1)
-        prep([("e", 1, 1024, 256, VL), ("e", 1, 1280, 256, VL)])
-        passes(2, "v", "e", 1, ms=(0, 1), n0=0, n=256)
-        passes(2, "v", "e", 1, ms=(0, 1), n0=256, n=256, stop=True)
-        passes(2, "v", "e", 1, ms=(2, 3), stop=True)
-        drain(2, 0, "s", 0, 256)
-        store(1024, 1280, 0, 1)
-        drain(2, 1, "v")
-        store(1024, 1536, 1, 2)
-        drain(2, 0, "s", 256, 256)
-        store(1280, 1536, 0, 1)
+        for m in (0, 1):
+            drain(2, m, "sv"[m % 2])
+        passes(1, "w", "dy", 0, ms=(0, 1), start=True)
+        passes(1, "w", "dy", 1, ms=(0, 1))
+        prep([("e", 0, c, 512, VW) for c in (0, 512)] + [("e", 0, c, 256, VH) for c in (1024, 1280)])
         drain(2, 2, "s")
-        store(1024, 1536, 2, 3)
-        drain(2, 3, "v")
-        store(1024, 1536, 3, 4)
+        for m in (2, 3):
+            one_pass(1, m, "w", "dy", 0, start=True)
+            one_pass(1, m, "w", "dy", 1)
+        prep([("e", 1, 0, 256, 192), ("e", 1, 256, 256, 160), ("e", 1, 512, 256, 128)])
+        prep([("v", 0, 0, 128, VQ), ("v", 0, 128, 128, VQ), ("v", 0, 256, 256, VH), ("e", 1, 768, 128, VH // 2)])
+        for m in range(4):
+            both(m)
+        prep([("v", 1, 0, 128, VQ), ("v", 1, 128, 128, VQ), ("v", 1, 256, 256, VH)])
+        for m in range(4):
+            close(m)
+        drain(0, 0, "s", 0, 256)
+        store(0, 256, 0, 1)
+        drain(1, 0, "v", 0, 384)
+        drain(0, 0, "s", 256, 256)
+        store(256, CUT, 0, 1)
+        drain(1, 0, "v", 384, 128)
+        for m in (1, 2, 3):
+            drain(0, m, "s")
+            drain(1, m, "v" if m < 3 else "s")
+            store(0, CUT, m, m + 1)
+        late_pass("a", 0, 0, 0, 1024, 256, True, False, at=128)
+        late_pass("b", 0, 4, 0, 1280, 256, True, False)
+        for m in (1, 2):
+            late_pass("a", m, m, 0, 1024, 512, True, False)
+        one_pass(2, 3, "w", "dy", 0, start=True, fresh=3)
+        one_pass(2, 3, "w", "dy", 1)
+        one_pass(2, 3, "v", "e", 0)
+        jobs = [interleave("e", 1, CUT, 128, 128), interleave("e", 1, 1024, 256, 256)]
+        quantise(jobs[0])
+        quantise(jobs[1])
+        jobs.append(interleave("e", 1, 1280, 256, VL))
+        late_pass("a", 0, 0, 1, CUT, 128, False, False)
+        late_pass("c", 3, 7, 1, CUT, 128, True, True)
+        late_pass("a", 0, 0, 1, 1024, 256, False, True, at=128)
+        one_pass(2, 3, "v", "e", 1, n0=0, n=256)
+        quantise(jobs[2])
+        late_pass("b", 0, 4, 1, 1280, 256, False, True)
+        one_pass(2, 3, "v", "e", 1, n0=256, n=256, stop=True)
+        add("a", 0, CUT, 384)
+        store(CUT, 1280, 0, 1)
+        add("b", 0, 1280, 256)
+        store(1280, 1536, 0, 1)
+        add("c", 3, CUT, 128)
+        drain(2, 3, "s")
+        store(CUT, 1536, 3, 4)
+        for m in (1, 2):
+            late_pass("a", m, m, 1, 1024, 512, False, True)
+            late_pass("c", m, 4 + m, 1, CUT, 128, True, True)
+            add("a", m, 1024, 512)
+            add("c", m, CUT, 128)
+            store(CUT, 1536, m, m + 1)

@@ -16,15 +16,14 @@ P = 128
 J = 4
 K_PASS = P * J
 CHUNK = 512
-VW = 248
-VH = 128
-VQ = 80
-VL = 96
-CUT = 896
+VW = 272
+VH = 144
+VQ = 64
+VL = 160
 
 
 def bank(c, m):
-    return m if c in (0, 3) else 4 + m
+    return {0: 2 * m, 1: 2 * m + 1, 2: 2 * m + 1, 3: 2}[c]
 
 
 def tile_mix_aux_fm_none_kernel(tc, w, dy, v, e, out):
@@ -32,20 +31,21 @@ def tile_mix_aux_fm_none_kernel(tc, w, dy, v, e, out):
     hbm = {"w": w, "dy": dy, "v": v, "e": e}
     fmt = {"w": E4M3, "dy": E5M2, "v": E4M3, "e": E4M3}
     loads = [
-        ("w", 0, 0, 512),
-        ("w", 1, 0, 512),
         ("dy", 0, 0, 1536),
+        ("w", 0, 0, 512),
         ("dy", 1, 0, 1536),
-        ("e", 0, 0, 1536),
-        ("e", 1, 0, 896),
+        ("w", 1, 0, 512),
+        ("e", 0, 0, 1024),
+        ("e", 1, 0, 1024),
         ("v", 0, 0, 512),
         ("v", 1, 0, 512),
-        ("e", 1, 896, 640),
+        ("e", 0, 1024, 512),
+        ("e", 1, 1024, 512),
     ]
 
     with ExitStack() as ctx:
         keep = ctx.enter_context(tc.tile_pool(name="keep", bufs=1))
-        stage = ctx.enter_context(tc.tile_pool(name="stage", bufs=6))
+        stage = ctx.enter_context(tc.tile_pool(name="stage", bufs=5))
         psum = ctx.enter_context(tc.psum_pool(name="psum", bufs=1))
         ctx.enter_context(tc.manual_schedule())
 
@@ -66,8 +66,8 @@ def tile_mix_aux_fm_none_kernel(tc, w, dy, v, e, out):
                 codes[name, g] = keep.tile([P, width], U32, name="codes_%s%d" % (name, g), align_bytes=64)
                 scales[name, g] = keep.tile([P, width], U8, name="scales_%s%d" % (name, g), align_bytes=64)
 
-        def interleave(name, g, c0, cols, v_cols):
-            b = stage.tile([P, cols, J], BF16, name="grouped", align_bytes=64)
+        def interleave(name, g, c0, cols, v_cols, tag="grouped"):
+            b = stage.tile([P, cols, J], BF16, name=tag, align_bytes=64)
             t, h = raw[name, g, c0]
             for copy, lo, hi in ((nc.vector.tensor_copy, 0, v_cols), (nc.scalar.copy, v_cols, cols)):
                 if hi > lo:
@@ -127,97 +127,90 @@ def tile_mix_aux_fm_none_kernel(tc, w, dy, v, e, out):
                 out=rows.rearrange("(m p) t -> p m t", p=P), in_=res[0][:, m0:m1, t0:t1]
             )
 
-        def close(m):
-            one_pass(0, m, "v", "e", 1, stop=True)
-            one_pass(1, m, "v", "e", 1, n0=0, n=256)
-            one_pass(1, m, "v", "e", 1, n0=256, n=128, stop=True)
-
-        def both(m):
+        def both(m, sta, mov, g, **kw):
             for c in (0, 1):
-                one_pass(c, m, "v", "e", 0)
+                one_pass(c, m, sta, mov, g, **kw)
 
-        def add(key, m, t0, n):
-            part = res[0][:, m, t0 : t0 + n]
-            nc.vector.tensor_tensor(out=part, in0=late[key, m][:, 0:n], in1=part, op=mybir.AluOpType.add)
+        def weights(g):
+            return [("v", g, 0, 128, VQ), ("v", g, 128, 128, VQ), ("v", g, 256, 256, VH)]
 
         late = {}
 
-        def late_pass(key, m, b, g, t0, n, start, stop, at=0):
-            if start:
-                late[key, m] = psum.tile([P, CHUNK], F32, name="bank%d" % b)
+        def late_pass(key, b, m, g, t0, n):
+            if g == 0:
+                late[key] = psum.tile([P, CHUNK], F32, name="bank%d" % b)
             rows = slice(m * P, (m + 1) * P)
             cols = slice(t0, t0 + n)
             nc.tensor.matmul_mx(
-                out=late[key, m][:, at : at + n],
+                out=late[key][:, 0:n],
                 lhsT=codes["v", g][:, rows].bitcast(E4M3),
                 lhsT_scale=scales["v", g][:, rows],
                 rhs=codes["e", g][:, cols].bitcast(E4M3),
                 rhs_scale=scales["e", g][:, cols],
-                start=start,
-                stop=stop,
+                start=g == 0,
+                stop=g == 1,
             )
 
-        prep([("w", 0, 0, 512, VW), ("w", 1, 0, 512, VW)])
-        prep([("dy", 0, c, 512, VW) for c in (0, 1024, 512)])
-        passes(0, "w", "dy", 0, start=True)
+        def add_store(key, m, t0, n):
+            part = res[0][:, m, t0 : t0 + n]
+            nc.vector.tensor_tensor(out=part, in0=late[key][:, 0:n], in1=part, op=mybir.AluOpType.add)
+            store(t0, t0 + n, m, m + 1)
+
+        prep([("dy", 0, c, 512, VW) for c in (0, 1024, 512)] + [("w", 0, 0, 256, VH), ("w", 0, 256, 128, VQ)])
+        held = interleave("w", 0, 384, 128, VQ, "held")
+        passes(0, "w", "dy", 0, ms=(0, 1, 2), start=True)
         passes(2, "w", "dy", 0, ms=(0, 1, 2), start=True)
-        prep([("dy", 1, c, 512, VW) for c in (1024, 0, 512)])
+        prep([("dy", 1, c, 512, VW) for c in (1024, 0, 512)] + [("w", 1, 0, 512, VW)])
         passes(2, "w", "dy", 1, ms=(0, 1, 2), stop=True)
-        passes(0, "w", "dy", 1)
-        for m in (0, 1):
+        passes(0, "w", "dy", 1, ms=(0, 1, 2))
+        for m in range(3):
             drain(2, m, "sv"[m % 2])
-        passes(1, "w", "dy", 0, ms=(0, 1), start=True)
-        passes(1, "w", "dy", 1, ms=(0, 1))
-        prep([("e", 0, c, 512, VW) for c in (0, 512)] + [("e", 0, c, 256, VH) for c in (1024, 1280)])
-        drain(2, 2, "s")
-        for m in (2, 3):
             one_pass(1, m, "w", "dy", 0, start=True)
             one_pass(1, m, "w", "dy", 1)
-        prep([("e", 1, 0, 256, 192), ("e", 1, 256, 256, 160), ("e", 1, 512, 256, 128)])
-        prep([("v", 0, 0, 128, VQ), ("v", 0, 128, 128, VQ), ("v", 0, 256, 256, VH), ("e", 1, 768, 128, VH // 2)])
+        prep([("e", 0, c, 512, VW) for c in (0, 512)])
+        first = interleave("e", 1, 0, 256, VH)
+        quantise(held)
+        both(3, "w", "dy", 0, start=True)
+        both(3, "w", "dy", 1)
+        second = interleave("e", 1, 256, 256, VH)
+        quantise(first)
+        third = interleave("e", 1, 512, 256, VH)
+        quantise(second)
+        quantise(third)
+        prep(weights(0) + [("e", 1, 768, 256, VH)])
         for m in range(4):
-            both(m)
-        prep([("v", 1, 0, 128, VQ), ("v", 1, 128, 128, VQ), ("v", 1, 256, 256, VH)])
+            both(m, "v", "e", 0)
+        prep(weights(1))
         for m in range(4):
-            close(m)
-        drain(0, 0, "s", 0, 256)
-        store(0, 256, 0, 1)
-        drain(1, 0, "v", 0, 384)
-        drain(0, 0, "s", 256, 256)
-        store(256, CUT, 0, 1)
-        drain(1, 0, "v", 384, 128)
-        for m in (1, 2, 3):
-            drain(0, m, "s")
-            drain(1, m, "v" if m < 3 else "s")
-            store(0, CUT, m, m + 1)
-        late_pass("a", 0, 0, 0, 1024, 256, True, False, at=128)
-        late_pass("b", 0, 4, 0, 1280, 256, True, False)
+            both(m, "v", "e", 1, stop=True)
+        drain(0, 0, "s")
+        drain(1, 0, "v")
+        store(0, 1024, 0, 1)
         for m in (1, 2):
-            late_pass("a", m, m, 0, 1024, 512, True, False)
+            drain(0, m, "s")
+            drain(1, m, "s")
+            store(0, 1024, m, m + 1)
+        prep([("e", 0, 1024, 256, 256), ("e", 0, 1280, 256, 256)])
+        drain(0, 3, "s")
+        drain(1, 3, "v")
+        store(0, 1024, 3, 4)
         one_pass(2, 3, "w", "dy", 0, start=True, fresh=3)
         one_pass(2, 3, "w", "dy", 1)
+        late_pass("a", 0, 0, 0, 1024, 256)
+        late_pass("b", 1, 0, 0, 1280, 256)
         one_pass(2, 3, "v", "e", 0)
-        jobs = [interleave("e", 1, CUT, 128, 128), interleave("e", 1, 1024, 256, 256)]
-        quantise(jobs[0])
-        quantise(jobs[1])
-        jobs.append(interleave("e", 1, 1280, 256, VL))
-        late_pass("a", 0, 0, 1, CUT, 128, False, False)
-        late_pass("c", 3, 7, 1, CUT, 128, True, True)
-        late_pass("a", 0, 0, 1, 1024, 256, False, True, at=128)
+        late_pass(1, 3, 1, 0, 1024, 512)
+        late_pass(2, 4, 2, 0, 1024, 512)
+        prep([("e", 1, 1024, 256, VL), ("e", 1, 1280, 256, VL)])
+        late_pass("a", 0, 0, 1, 1024, 256)
         one_pass(2, 3, "v", "e", 1, n0=0, n=256)
-        quantise(jobs[2])
-        late_pass("b", 0, 4, 1, 1280, 256, False, True)
+        late_pass("b", 1, 0, 1, 1280, 256)
         one_pass(2, 3, "v", "e", 1, n0=256, n=256, stop=True)
-        add("a", 0, CUT, 384)
-        store(CUT, 1280, 0, 1)
-        add("b", 0, 1280, 256)
-        store(1280, 1536, 0, 1)
-        add("c", 3, CUT, 128)
+        late_pass(1, 3, 1, 1, 1024, 512)
+        late_pass(2, 4, 2, 1, 1024, 512)
+        add_store("a", 0, 1024, 256)
+        add_store("b", 0, 1280, 256)
         drain(2, 3, "s")
-        store(CUT, 1536, 3, 4)
-        for m in (1, 2):
-            late_pass("a", m, m, 1, 1024, 512, False, True)
-            late_pass("c", m, 4 + m, 1, CUT, 128, True, True)
-            add("a", m, 1024, 512)
-            add("c", m, CUT, 128)
-            store(CUT, 1536, m, m + 1)
+        store(1024, 1536, 3, 4)
+        add_store(1, 1, 1024, 512)
+        add_store(2, 2, 1024, 512)

@@ -16,32 +16,18 @@ P = 128
 J = 4
 K_PASS = P * J
 CHUNK = 512
+HALF = 256
+CUT = 1024
 VW = 272
 VH = 144
 VQ = 64
 VL = 160
 
 
-def bank(c, m):
-    return {0: 2 * m, 1: 2 * m + 1, 2: 2 * m + 1, 3: 2}[c]
-
-
 def tile_mix_aux_fm_none_kernel(tc, w, dy, v, e, out):
     nc = tc.nc
     hbm = {"w": w, "dy": dy, "v": v, "e": e}
     fmt = {"w": E4M3, "dy": E5M2, "v": E4M3, "e": E4M3}
-    loads = [
-        ("dy", 0, 0, 1536),
-        ("w", 0, 0, 512),
-        ("dy", 1, 0, 1536),
-        ("w", 1, 0, 512),
-        ("e", 0, 0, 1024),
-        ("e", 1, 0, 1024),
-        ("v", 0, 0, 512),
-        ("v", 1, 0, 512),
-        ("e", 0, 1024, 512),
-        ("e", 1, 1024, 512),
-    ]
 
     with ExitStack() as ctx:
         keep = ctx.enter_context(tc.tile_pool(name="keep", bufs=1))
@@ -50,14 +36,31 @@ def tile_mix_aux_fm_none_kernel(tc, w, dy, v, e, out):
         ctx.enter_context(tc.manual_schedule())
 
         raw = {}
-        for name, g, c0, cols in loads:
+
+        def load(name, g, c0, cols):
             t = keep.tile([P, J, cols], F32, name="raw_%s%d_%d" % (name, g, c0))
-            nc.sync.dma_start(
-                out=t[:],
-                in_=hbm[name][g * K_PASS : (g + 1) * K_PASS, c0 : c0 + cols].rearrange("(p j) c -> p j c", j=J),
-            )
+            rows = hbm[name][g * K_PASS : (g + 1) * K_PASS, c0 : c0 + cols]
+            nc.sync.dma_start(out=t[:], in_=rows.rearrange("(p j) c -> p j c", j=J))
             for c in range(0, cols, P):
                 raw[name, g, c0 + c] = (t, c)
+
+        def load_both(name):
+            cols = hbm[name].shape[1]
+            t = keep.tile([P, 2, J * cols], F32, name="raw_%s" % name)
+            nc.sync.dma_start(out=t[:], in_=hbm[name][:, :].rearrange("(g p j) c -> p g (j c)", g=2, j=J))
+            for g in range(2):
+                for c in range(0, cols, P):
+                    raw[name, g, c] = (t[:, g, :].rearrange("p (j c) -> p j c", j=J), c)
+
+        load("dy", 0, 0, T)
+        load("dy", 1, 0, T)
+        load_both("w")
+        load("e", 0, 0, CUT)
+        load("e", 1, 0, CUT)
+        load("v", 0, 0, M)
+        load("v", 1, 0, M)
+        load("e", 0, CUT, T - CUT)
+        load("e", 1, CUT, T - CUT)
 
         codes, scales = {}, {}
         for name in ("w", "dy", "v", "e"):
@@ -65,6 +68,7 @@ def tile_mix_aux_fm_none_kernel(tc, w, dy, v, e, out):
             for g in range(2):
                 codes[name, g] = keep.tile([P, width], U32, name="codes_%s%d" % (name, g), align_bytes=64)
                 scales[name, g] = keep.tile([P, width], U8, name="scales_%s%d" % (name, g), align_bytes=64)
+        res = keep.tile([P, M // P, T], F32, name="res")
 
         def interleave(name, g, c0, cols, v_cols, tag="grouped"):
             b = stage.tile([P, cols, J], BF16, name=tag, align_bytes=64)
@@ -94,15 +98,19 @@ def tile_mix_aux_fm_none_kernel(tc, w, dy, v, e, out):
                 last = job
             quantise(last)
 
+        def v_parts(g):
+            return [("v", g, 0, P, VQ), ("v", g, P, P, VQ), ("v", g, HALF, HALF, VH)]
+
         acc = {}
 
-        def one_pass(c, m, sta, mov, g, start=False, stop=False, n0=0, n=CHUNK, fresh=None):
-            if start:
-                acc[c, m] = psum.tile([P, CHUNK], F32, name="bank%d" % bank(c if fresh is None else fresh, m))
+        def open_sum(m, t0, bank):
+            acc[m, t0] = psum.tile([P, CHUNK], F32, name="bank%d" % bank)
+
+        def mm(m, t0, sta, mov, g, start=False, stop=False, n0=0, n=CHUNK):
             rows = slice(m * P, (m + 1) * P)
-            cols = slice(c * CHUNK + n0, c * CHUNK + n0 + n)
+            cols = slice(t0 + n0, t0 + n0 + n)
             nc.tensor.matmul_mx(
-                out=acc[c, m][:, n0 : n0 + n],
+                out=acc[m, t0][:, n0 : n0 + n],
                 lhsT=codes[sta, g][:, rows].bitcast(fmt[sta]),
                 lhsT_scale=scales[sta, g][:, rows],
                 rhs=codes[mov, g][:, cols].bitcast(fmt[mov]),
@@ -111,106 +119,86 @@ def tile_mix_aux_fm_none_kernel(tc, w, dy, v, e, out):
                 stop=stop,
             )
 
-        def passes(c, sta, mov, g, ms=range(M // P), **kw):
-            for m in ms:
-                one_pass(c, m, sta, mov, g, **kw)
+        def dy_sum(m, t0, bank, stop=False):
+            open_sum(m, t0, bank)
+            mm(m, t0, "w", "dy", 0, start=True)
+            mm(m, t0, "w", "dy", 1, stop=stop)
 
-        res = [keep.tile([P, M // P, T], F32, name="res")]
+        def drain(copy, m, t0):
+            copy(out=res[:, m, t0 : t0 + CHUNK], in_=acc[m, t0][:])
 
-        def drain(c, m, eng, n0=0, n=CHUNK):
-            copy = nc.vector.tensor_copy if eng == "v" else nc.scalar.copy
-            copy(out=res[0][:, m, c * CHUNK + n0 : c * CHUNK + n0 + n], in_=acc[c, m][:, n0 : n0 + n])
+        def add(m, t0, n):
+            part = res[:, m, t0 : t0 + n]
+            nc.vector.tensor_tensor(out=part, in0=acc[m, t0][:, 0:n], in1=part, op=mybir.AluOpType.add)
 
-        def store(t0, t1, m0, m1):
+        def store(m0, m1, t0, t1):
             rows = out[m0 * P : m1 * P, t0:t1]
-            nc.sync.dma_start(
-                out=rows.rearrange("(m p) t -> p m t", p=P), in_=res[0][:, m0:m1, t0:t1]
-            )
+            nc.sync.dma_start(out=rows.rearrange("(m p) t -> p m t", p=P), in_=res[:, m0:m1, t0:t1])
 
-        def both(m, sta, mov, g, **kw):
-            for c in (0, 1):
-                one_pass(c, m, sta, mov, g, **kw)
+        on_v, on_s = nc.vector.tensor_copy, nc.scalar.copy
 
-        def weights(g):
-            return [("v", g, 0, 128, VQ), ("v", g, 128, 128, VQ), ("v", g, 256, 256, VH)]
+        for g in range(2):
+            prep([("dy", g, c, CHUNK, VW) for c in range(0, T, CHUNK)])
+        prep([("w", 0, 0, HALF, VH), ("w", 0, HALF, P, VQ), ("w", 1, 0, M, VW)])
+        held = interleave("w", 0, HALF + P, P, VQ, "held")
+        for m in (0, 1):
+            dy_sum(m, CUT, 2 * m + 1, stop=True)
+        for m in (0, 1, 2):
+            dy_sum(m, 0, 2 * m)
+        dy_sum(2, CHUNK, 5)
+        for m, copy in ((0, on_s), (1, on_v)):
+            drain(copy, m, CUT)
+            dy_sum(m, CHUNK, 2 * m + 1)
+        prep([("e", 0, c, CHUNK, VW) for c in (0, CHUNK)])
 
-        late = {}
-
-        def late_pass(key, b, m, g, t0, n):
-            if g == 0:
-                late[key] = psum.tile([P, CHUNK], F32, name="bank%d" % b)
-            rows = slice(m * P, (m + 1) * P)
-            cols = slice(t0, t0 + n)
-            nc.tensor.matmul_mx(
-                out=late[key][:, 0:n],
-                lhsT=codes["v", g][:, rows].bitcast(E4M3),
-                lhsT_scale=scales["v", g][:, rows],
-                rhs=codes["e", g][:, cols].bitcast(E4M3),
-                rhs_scale=scales["e", g][:, cols],
-                start=g == 0,
-                stop=g == 1,
-            )
-
-        def add_store(key, m, t0, n):
-            part = res[0][:, m, t0 : t0 + n]
-            nc.vector.tensor_tensor(out=part, in0=late[key][:, 0:n], in1=part, op=mybir.AluOpType.add)
-            store(t0, t0 + n, m, m + 1)
-
-        prep([("dy", 0, c, 512, VW) for c in (0, 1024, 512)] + [("w", 0, 0, 256, VH), ("w", 0, 256, 128, VQ)])
-        held = interleave("w", 0, 384, 128, VQ, "held")
-        passes(0, "w", "dy", 0, ms=(0, 1, 2), start=True)
-        passes(2, "w", "dy", 0, ms=(0, 1, 2), start=True)
-        prep([("dy", 1, c, 512, VW) for c in (1024, 0, 512)] + [("w", 1, 0, 512, VW)])
-        passes(2, "w", "dy", 1, ms=(0, 1, 2), stop=True)
-        passes(0, "w", "dy", 1, ms=(0, 1, 2))
-        for m in range(3):
-            drain(2, m, "sv"[m % 2])
-            one_pass(1, m, "w", "dy", 0, start=True)
-            one_pass(1, m, "w", "dy", 1)
-        prep([("e", 0, c, 512, VW) for c in (0, 512)])
-        first = interleave("e", 1, 0, 256, VH)
+        jobs = [interleave("e", 1, 0, HALF, VH)]
         quantise(held)
-        both(3, "w", "dy", 0, start=True)
-        both(3, "w", "dy", 1)
-        second = interleave("e", 1, 256, 256, VH)
-        quantise(first)
-        third = interleave("e", 1, 512, 256, VH)
-        quantise(second)
-        quantise(third)
-        prep(weights(0) + [("e", 1, 768, 256, VH)])
+        dy_sum(3, 0, 6)
+        dy_sum(3, CHUNK, 7)
+        for c in (HALF, CHUNK):
+            jobs.append(interleave("e", 1, c, HALF, VH))
+            quantise(jobs[-2])
+        quantise(jobs[-1])
+        prep(v_parts(0) + [("e", 1, CHUNK + HALF, HALF, VH)])
         for m in range(4):
-            both(m, "v", "e", 0)
-        prep(weights(1))
+            for t0 in (0, CHUNK):
+                mm(m, t0, "v", "e", 0)
+        prep(v_parts(1))
         for m in range(4):
-            both(m, "v", "e", 1, stop=True)
-        drain(0, 0, "s")
-        drain(1, 0, "v")
-        store(0, 1024, 0, 1)
+            for t0 in (0, CHUNK):
+                mm(m, t0, "v", "e", 1, stop=True)
+
+        drain(on_s, 0, 0)
+        drain(on_v, 0, CHUNK)
+        store(0, 1, 0, CUT)
         for m in (1, 2):
-            drain(0, m, "s")
-            drain(1, m, "s")
-            store(0, 1024, m, m + 1)
-        prep([("e", 0, 1024, 256, 256), ("e", 0, 1280, 256, 256)])
-        drain(0, 3, "s")
-        drain(1, 3, "v")
-        store(0, 1024, 3, 4)
-        one_pass(2, 3, "w", "dy", 0, start=True, fresh=3)
-        one_pass(2, 3, "w", "dy", 1)
-        late_pass("a", 0, 0, 0, 1024, 256)
-        late_pass("b", 1, 0, 0, 1280, 256)
-        one_pass(2, 3, "v", "e", 0)
-        late_pass(1, 3, 1, 0, 1024, 512)
-        late_pass(2, 4, 2, 0, 1024, 512)
-        prep([("e", 1, 1024, 256, VL), ("e", 1, 1280, 256, VL)])
-        late_pass("a", 0, 0, 1, 1024, 256)
-        one_pass(2, 3, "v", "e", 1, n0=0, n=256)
-        late_pass("b", 1, 0, 1, 1280, 256)
-        one_pass(2, 3, "v", "e", 1, n0=256, n=256, stop=True)
-        late_pass(1, 3, 1, 1, 1024, 512)
-        late_pass(2, 4, 2, 1, 1024, 512)
-        add_store("a", 0, 1024, 256)
-        add_store("b", 0, 1280, 256)
-        drain(2, 3, "s")
-        store(1024, 1536, 3, 4)
-        add_store(1, 1, 1024, 512)
-        add_store(2, 2, 1024, 512)
+            drain(on_s, m, 0)
+            drain(on_s, m, CHUNK)
+        store(1, 2, 0, CUT)
+        prep([("e", 0, c, HALF, HALF) for c in (CUT, CUT + HALF)])
+        drain(on_s, 3, 0)
+        drain(on_v, 3, CHUNK)
+        store(2, 4, 0, CUT)
+
+        halves = (CUT, CUT + HALF)
+        for m in (2, 3):
+            dy_sum(m, CUT, m - 2)
+        for h, t0 in enumerate(halves):
+            for m in (0, 1):
+                open_sum(m, t0, 2 + 2 * h + m)
+                mm(m, t0, "v", "e", 0, start=True, n=HALF)
+        for m in (2, 3):
+            mm(m, CUT, "v", "e", 0)
+        prep([("e", 1, c, HALF, VL) for c in halves])
+        for t0 in halves:
+            for m in (0, 1):
+                mm(m, t0, "v", "e", 1, stop=True, n=HALF)
+        for m in (2, 3):
+            mm(m, CUT, "v", "e", 1, stop=True)
+        for t0 in halves:
+            for m in (0, 1):
+                add(m, t0, HALF)
+            store(0, 2, t0, t0 + HALF)
+        drain(on_s, 2, CUT)
+        drain(on_v, 3, CUT)
+        store(2, 4, CUT, T)

@@ -184,21 +184,24 @@ def tile_mix_aux_fm_none_kernel(tc, w, dy, v, e, out):
         for m in (2, 3):
             dy_sum(m, CUT, m - 2)
         for h, t0 in enumerate(halves):
-            for m in (0, 1):
-                open_sum(m, t0, 2 + 2 * h + m)
-                mm(m, t0, "v", "e", 0, start=True, n=HALF)
+            open_sum(0, t0, 2 + h)
+            mm(0, t0, "v", "e", 0, start=True, n=HALF)
+        open_sum(1, CUT, 4)
+        mm(1, CUT, "v", "e", 0, start=True)
         for m in (2, 3):
             mm(m, CUT, "v", "e", 0)
         prep([("e", 1, c, HALF, VL) for c in halves])
-        for t0 in halves:
-            for m in (0, 1):
-                mm(m, t0, "v", "e", 1, stop=True, n=HALF)
+        mm(0, CUT, "v", "e", 1, stop=True, n=HALF)
+        mm(1, CUT, "v", "e", 1, n=HALF)
+        mm(0, CUT + HALF, "v", "e", 1, stop=True, n=HALF)
+        mm(1, CUT, "v", "e", 1, stop=True, n0=HALF, n=HALF)
         for m in (2, 3):
             mm(m, CUT, "v", "e", 1, stop=True)
         for t0 in halves:
-            for m in (0, 1):
-                add(m, t0, HALF)
-            store(0, 2, t0, t0 + HALF)
+            add(0, t0, HALF)
+        store(0, 1, CUT, T)
+        add(1, CUT, CHUNK)
+        store(1, 2, CUT, T)
         drain(on_s, 2, CUT)
         drain(on_v, 3, CUT)
         store(2, 4, CUT, T)

@@ -76,8 +76,8 @@ def tile_mix_aux_fm_none_kernel(tc, w, dy, v, e, out):
             for copy, lo, hi in ((nc.vector.tensor_copy, 0, v_cols), (nc.scalar.copy, v_cols, cols)):
                 if hi > lo:
                     copy(
-                        out=b[:, lo:hi, :].rearrange("p (c i) j -> p c j i", i=2),
-                        in_=t[:, :, h + lo : h + hi].rearrange("p j (c i) -> p c j i", i=2),
+                        out=b[:, lo:hi, :].rearrange("p (c i) j -> p c j i", i=4),
+                        in_=t[:, :, h + lo : h + hi].rearrange("p j (c i) -> p c j i", i=4),
                     )
             return (name, g, c0, cols, b)
 

@@ -22,6 +22,7 @@ VW = 272
 VH = 144
 VQ = 64
 VL = 160
+DMA_ALIGN = 256
 
 
 def tile_mix_aux_fm_none_kernel(tc, w, dy, v, e, out):
@@ -38,7 +39,7 @@ def tile_mix_aux_fm_none_kernel(tc, w, dy, v, e, out):
         raw = {}
 
         def load(name, g, c0, cols):
-            t = keep.tile([P, J, cols], F32, name="raw_%s%d_%d" % (name, g, c0))
+            t = keep.tile([P, J, cols], F32, name="raw_%s%d_%d" % (name, g, c0), align_bytes=DMA_ALIGN)
             rows = hbm[name][g * K_PASS : (g + 1) * K_PASS, c0 : c0 + cols]
             nc.sync.dma_start(out=t[:], in_=rows.rearrange("(p j) c -> p j c", j=J))
             for c in range(0, cols, P):
@@ -46,7 +47,7 @@ def tile_mix_aux_fm_none_kernel(tc, w, dy, v, e, out):
 
         def load_both(name):
             cols = hbm[name].shape[1]
-            t = keep.tile([P, 2, J * cols], F32, name="raw_%s" % name)
+            t = keep.tile([P, 2, J * cols], F32, name="raw_%s" % name, align_bytes=DMA_ALIGN)
             nc.sync.dma_start(out=t[:], in_=hbm[name][:, :].rearrange("(g p j) c -> p g (j c)", g=2, j=J))
             for g in range(2):
                 for c in range(0, cols, P):
@@ -68,7 +69,7 @@ def tile_mix_aux_fm_none_kernel(tc, w, dy, v, e, out):
             for g in range(2):
                 codes[name, g] = keep.tile([P, width], U32, name="codes_%s%d" % (name, g), align_bytes=64)
                 scales[name, g] = keep.tile([P, width], U8, name="scales_%s%d" % (name, g), align_bytes=64)
-        res = keep.tile([P, M // P, T], F32, name="res")
+        res = keep.tile([P, M // P, T], F32, name="res", align_bytes=DMA_ALIGN)
 
         def interleave(name, g, c0, cols, v_cols, tag="grouped"):
             b = stage.tile([P, cols, J], BF16, name=tag, align_bytes=64)

@@ -22,7 +22,7 @@ VW = 272
 VH = 144
 VQ = 64
 VL = 160
-DMA_ALIGN = 256
+DMA_ALIGN = 2048
 
 
 def tile_mix_aux_fm_none_kernel(tc, w, dy, v, e, out):

@@ -17,12 +17,8 @@ J = 4
 K_PASS = P * J
 CHUNK = 512
 HALF = 256
-CUT = 1024
-VW = 272
-VH = 144
-VQ = 64
-VL = 160
-DMA_ALIGN = 2048
+EARLY = 1024
+DMA_ALIGN = 256
 
 
 def tile_mix_aux_fm_none_kernel(tc, w, dy, v, e, out):
@@ -36,49 +32,59 @@ def tile_mix_aux_fm_none_kernel(tc, w, dy, v, e, out):
         psum = ctx.enter_context(tc.psum_pool(name="psum", bufs=1))
         ctx.enter_context(tc.manual_schedule())
 
-        raw = {}
-
-        def load(name, g, c0, cols):
-            t = keep.tile([P, J, cols], F32, name="raw_%s%d_%d" % (name, g, c0), align_bytes=DMA_ALIGN)
-            rows = hbm[name][g * K_PASS : (g + 1) * K_PASS, c0 : c0 + cols]
-            nc.sync.dma_start(out=t[:], in_=rows.rearrange("(p j) c -> p j c", j=J))
-            for c in range(0, cols, P):
-                raw[name, g, c0 + c] = (t, c)
-
-        def load_both(name):
-            cols = hbm[name].shape[1]
-            t = keep.tile([P, 2, J * cols], F32, name="raw_%s" % name, align_bytes=DMA_ALIGN)
-            nc.sync.dma_start(out=t[:], in_=hbm[name][:, :].rearrange("(g p j) c -> p g (j c)", g=2, j=J))
-            for g in range(2):
-                for c in range(0, cols, P):
-                    raw[name, g, c] = (t[:, g, :].rearrange("p (j c) -> p j c", j=J), c)
-
-        load("dy", 0, 0, T)
-        load("dy", 1, 0, T)
-        load_both("w")
-        load("e", 0, 0, CUT)
-        load("e", 1, 0, CUT)
-        load("v", 0, 0, M)
-        load("v", 1, 0, M)
-        load("e", 0, CUT, T - CUT)
-        load("e", 1, CUT, T - CUT)
-
         codes, scales = {}, {}
-        for name in ("w", "dy", "v", "e"):
+        for name in ("dy", "e", "w", "v"):
             width = hbm[name].shape[1]
             for g in range(2):
                 codes[name, g] = keep.tile([P, width], U32, name="codes_%s%d" % (name, g), align_bytes=64)
                 scales[name, g] = keep.tile([P, width], U8, name="scales_%s%d" % (name, g), align_bytes=64)
         res = keep.tile([P, M // P, T], F32, name="res", align_bytes=DMA_ALIGN)
 
-        def interleave(name, g, c0, cols, v_cols, tag="grouped"):
-            b = stage.tile([P, cols, J], BF16, name=tag, align_bytes=64)
-            t, h = raw[name, g, c0]
+        def raw_tile(label, rows, cols):
+            t = keep.tile([P, rows * cols], F32, name="raw_" + label, align_bytes=DMA_ALIGN)
+            return t[:].rearrange("p (j c) -> p j c", j=rows)
+
+        def load(dst, name, g, runs, lo, hi):
+            rows = hbm[name][g * K_PASS : (g + 1) * K_PASS, :]
+            src = rows.rearrange("(p r j) c -> p r (j c)", p=P, r=runs)
+            nc.sync.dma_start(out=dst, in_=src[:, :, lo:hi])
+
+        def runs_of(t, runs):
+            return t.rearrange("p (r j) c -> p r (j c)", r=runs)
+
+        raw = {}
+
+        def load_both(name):
+            t = raw_tile(name, 2 * J, M)
+            nc.sync.dma_start(out=runs_of(t, 2), in_=hbm[name][:, :].rearrange("(g p j) c -> p g (j c)", g=2, j=J))
+            for g in range(2):
+                raw[name, g, 0] = (t[:, g * J : (g + 1) * J, :], 0)
+
+        def load_cols(name, g, lo, hi):
+            t = raw_tile("%s%d_%d" % (name, g, lo), J, hi - lo)
+            load(t, name, g, J, lo, hi)
+            raw[name, g, lo] = (t, lo)
+
+        load_both("w")
+        load_cols("dy", 0, 0, EARLY)
+        load_cols("dy", 1, 0, EARLY)
+        load_both("v")
+        load_cols("e", 0, 0, EARLY)
+        load_cols("e", 1, 0, EARLY)
+        load_cols("dy", 0, EARLY, T)
+        load_cols("dy", 1, EARLY, T)
+        load_cols("e", 0, EARLY, T)
+        load_cols("e", 1, EARLY, EARLY + HALF)
+        load_cols("e", 1, EARLY + HALF, T)
+
+        def interleave(name, g, c0, cols, v_cols):
+            b = stage.tile([P, cols, J], BF16, name="grouped", align_bytes=64)
+            t, first = raw[name, g, max(c for (n, h, c) in raw if (n, h) == (name, g) and c <= c0)]
             for copy, lo, hi in ((nc.vector.tensor_copy, 0, v_cols), (nc.scalar.copy, v_cols, cols)):
                 if hi > lo:
                     copy(
                         out=b[:, lo:hi, :].rearrange("p (c i) j -> p c j i", i=4),
-                        in_=t[:, :, h + lo : h + hi].rearrange("p j (c i) -> p c j i", i=4),
+                        in_=t[:, :, c0 - first + lo : c0 - first + hi].rearrange("p j (c i) -> p c j i", i=4),
                     )
             return (name, g, c0, cols, b)
 
@@ -99,9 +105,6 @@ def tile_mix_aux_fm_none_kernel(tc, w, dy, v, e, out):
                 last = job
             quantise(last)
 
-        def v_parts(g):
-            return [("v", g, 0, P, VQ), ("v", g, P, P, VQ), ("v", g, HALF, HALF, VH)]
-
         acc = {}
 
         def open_sum(m, t0, bank):
@@ -120,17 +123,8 @@ def tile_mix_aux_fm_none_kernel(tc, w, dy, v, e, out):
                 stop=stop,
             )
 
-        def dy_sum(m, t0, bank, stop=False):
-            open_sum(m, t0, bank)
-            mm(m, t0, "w", "dy", 0, start=True)
-            mm(m, t0, "w", "dy", 1, stop=stop)
-
-        def drain(copy, m, t0):
-            copy(out=res[:, m, t0 : t0 + CHUNK], in_=acc[m, t0][:])
-
-        def add(m, t0, n):
-            part = res[:, m, t0 : t0 + n]
-            nc.vector.tensor_tensor(out=part, in0=acc[m, t0][:, 0:n], in1=part, op=mybir.AluOpType.add)
+        def drain(copy, m, t0, n=CHUNK):
+            copy(out=res[:, m, t0 : t0 + n], in_=acc[m, t0][:, 0:n])
 
         def store(m0, m1, t0, t1):
             rows = out[m0 * P : m1 * P, t0:t1]
@@ -138,71 +132,55 @@ def tile_mix_aux_fm_none_kernel(tc, w, dy, v, e, out):
 
         on_v, on_s = nc.vector.tensor_copy, nc.scalar.copy
 
-        for g in range(2):
-            prep([("dy", g, c, CHUNK, VW) for c in range(0, T, CHUNK)])
-        prep([("w", 0, 0, HALF, VH), ("w", 0, HALF, P, VQ), ("w", 1, 0, M, VW)])
-        held = interleave("w", 0, HALF + P, P, VQ, "held")
-        for m in (0, 1):
-            dy_sum(m, CUT, 2 * m + 1, stop=True)
-        for m in (0, 1, 2):
-            dy_sum(m, 0, 2 * m)
-        dy_sum(2, CHUNK, 5)
-        for m, copy in ((0, on_s), (1, on_v)):
-            drain(copy, m, CUT)
-            dy_sum(m, CHUNK, 2 * m + 1)
-        prep([("e", 0, c, CHUNK, VW) for c in (0, CHUNK)])
+        early = [(m, t0) for t0 in (0, CHUNK) for m in range(4)]
+        halves = (EARLY, EARLY + HALF)
+        quarters = range(0, EARLY, HALF)
+        prep([("w", g, 0, M, 272) for g in range(2)])
+        prep([("dy", 0, c, CHUNK, 272) for c in (0, CHUNK)])
+        for bank, (m, t0) in enumerate(early):
+            open_sum(m, t0, bank)
+            mm(m, t0, "w", "dy", 0, start=True)
+        prep([("dy", 1, c, CHUNK, 272) for c in (0, CHUNK)])
+        for m, t0 in early:
+            mm(m, t0, "w", "dy", 1)
+        prep([("v", g, 0, M, 272) for g in range(2)])
+        prep([("e", 0, c, HALF, 136) for c in quarters])
+        for m, t0 in early:
+            mm(m, t0, "v", "e", 0)
+        prep([("e", 1, c, HALF, 136) for c in quarters])
+        for m, t0 in early:
+            mm(m, t0, "v", "e", 1, stop=True)
 
-        jobs = [interleave("e", 1, 0, HALF, VH)]
-        quantise(held)
-        dy_sum(3, 0, 6)
-        dy_sum(3, CHUNK, 7)
-        for c in (HALF, CHUNK):
-            jobs.append(interleave("e", 1, c, HALF, VH))
-            quantise(jobs[-2])
-        quantise(jobs[-1])
-        prep(v_parts(0) + [("e", 1, CHUNK + HALF, HALF, VH)])
-        for m in range(4):
-            for t0 in (0, CHUNK):
-                mm(m, t0, "v", "e", 0)
-        prep(v_parts(1))
-        for m in range(4):
-            for t0 in (0, CHUNK):
-                mm(m, t0, "v", "e", 1, stop=True)
-
-        drain(on_s, 0, 0)
-        drain(on_v, 0, CHUNK)
-        store(0, 1, 0, CUT)
-        for m in (1, 2):
-            drain(on_s, m, 0)
-            drain(on_s, m, CHUNK)
-        store(1, 2, 0, CUT)
-        prep([("e", 0, c, HALF, HALF) for c in (CUT, CUT + HALF)])
-        drain(on_s, 3, 0)
-        drain(on_v, 3, CHUNK)
-        store(2, 4, 0, CUT)
-
-        halves = (CUT, CUT + HALF)
-        for m in (2, 3):
-            dy_sum(m, CUT, m - 2)
-        for h, t0 in enumerate(halves):
-            open_sum(0, t0, 2 + h)
-            mm(0, t0, "v", "e", 0, start=True, n=HALF)
-        open_sum(1, CUT, 4)
-        mm(1, CUT, "v", "e", 0, start=True)
-        for m in (2, 3):
-            mm(m, CUT, "v", "e", 0)
-        prep([("e", 1, c, HALF, VL) for c in halves])
-        mm(0, CUT, "v", "e", 1, stop=True, n=HALF)
-        mm(1, CUT, "v", "e", 1, n=HALF)
-        mm(0, CUT + HALF, "v", "e", 1, stop=True, n=HALF)
-        mm(1, CUT, "v", "e", 1, stop=True, n0=HALF, n=HALF)
-        for m in (2, 3):
-            mm(m, CUT, "v", "e", 1, stop=True)
-        for t0 in halves:
-            add(0, t0, HALF)
-        store(0, 1, CUT, T)
-        add(1, CUT, CHUNK)
-        store(1, 2, CUT, T)
-        drain(on_s, 2, CUT)
-        drain(on_v, 3, CUT)
-        store(2, 4, CUT, T)
+        late = [(0, EARLY, HALF), (0, EARLY + HALF, HALF), (1, EARLY, CHUNK), (2, EARLY, CHUNK), (3, EARLY, CHUNK)]
+        prep([("dy", 0, c, HALF, HALF) for c in halves])
+        for m, t0 in early[0:4]:
+            drain(on_s, m, t0)
+        prep([("dy", 1, c, HALF, HALF) for c in halves])
+        for m, t0 in early[4:8]:
+            drain(on_s, m, t0)
+        for bank, (m, t0, n) in enumerate(late):
+            open_sum(m, t0, bank)
+            mm(m, t0, "w", "dy", 0, start=True, n=n)
+        for m, t0, n in late:
+            mm(m, t0, "w", "dy", 1, n=n)
+        store(0, 2, 0, EARLY)
+        store(2, 4, 0, EARLY)
+        prep([("e", 0, EARLY, HALF, HALF), ("e", 0, EARLY + HALF, HALF, 96)])
+        for m, t0, n in late:
+            mm(m, t0, "v", "e", 0, n=n)
+        prep([("e", 1, EARLY, P, 84), ("e", 1, EARLY + P, P, 64)])
+        mm(0, EARLY, "v", "e", 1, stop=True, n=HALF)
+        for m in (1, 2, 3):
+            mm(m, EARLY, "v", "e", 1, n=HALF)
+        prep([("e", 1, EARLY + HALF, P, 84), ("e", 1, EARLY + HALF + P, P, 64)])
+        drain(on_s, 0, EARLY, HALF)
+        mm(0, EARLY + HALF, "v", "e", 1, stop=True, n=HALF)
+        for m in (1, 2, 3):
+            mm(m, EARLY, "v", "e", 1, stop=True, n0=HALF, n=HALF)
+        drain(on_v, 0, EARLY + HALF, HALF)
+        store(0, 1, EARLY, T)
+        drain(on_s, 1, EARLY)
+        store(1, 2, EARLY, T)
+        drain(on_v, 2, EARLY)
+        drain(on_s, 3, EARLY)
+        store(2, 4, EARLY, T)

@@ -65,20 +65,19 @@ def tile_mix_aux_fm_none_kernel(tc, w, dy, v, e, out):
             load(t, name, g, J, lo, hi)
             raw[name, g, lo] = (t, lo)
 
+        load_cols("dy", 0, 0, T)
         load_both("w")
-        load_cols("dy", 0, 0, EARLY)
         load_cols("dy", 1, 0, EARLY)
-        load_both("v")
+        load_cols("v", 0, 0, M)
         load_cols("e", 0, 0, EARLY)
         load_cols("e", 1, 0, EARLY)
-        load_cols("dy", 0, EARLY, T)
+        load_cols("v", 1, 0, M)
         load_cols("dy", 1, EARLY, T)
         load_cols("e", 0, EARLY, T)
-        load_cols("e", 1, EARLY, EARLY + HALF)
-        load_cols("e", 1, EARLY + HALF, T)
+        load_cols("e", 1, EARLY, T)
 
-        def interleave(name, g, c0, cols, v_cols):
-            b = stage.tile([P, cols, J], BF16, name="grouped", align_bytes=64)
+        def interleave(name, g, c0, cols, v_cols, tag="grouped"):
+            b = stage.tile([P, cols, J], BF16, name=tag, align_bytes=64)
             t, first = raw[name, g, max(c for (n, h, c) in raw if (n, h) == (name, g) and c <= c0)]
             for copy, lo, hi in ((nc.vector.tensor_copy, 0, v_cols), (nc.scalar.copy, v_cols, cols)):
                 if hi > lo:
@@ -132,52 +131,67 @@ def tile_mix_aux_fm_none_kernel(tc, w, dy, v, e, out):
 
         on_v, on_s = nc.vector.tensor_copy, nc.scalar.copy
 
-        early = [(m, t0) for t0 in (0, CHUNK) for m in range(4)]
+        early = [(m, t0) for m in range(4) for t0 in (0, CHUNK)]
         halves = (EARLY, EARLY + HALF)
         quarters = range(0, EARLY, HALF)
+        prep([("dy", 0, c, CHUNK, 272) for c in range(0, T, CHUNK)])
         prep([("w", g, 0, M, 272) for g in range(2)])
-        prep([("dy", 0, c, CHUNK, 272) for c in (0, CHUNK)])
         for bank, (m, t0) in enumerate(early):
             open_sum(m, t0, bank)
             mm(m, t0, "w", "dy", 0, start=True)
         prep([("dy", 1, c, CHUNK, 272) for c in (0, CHUNK)])
         for m, t0 in early:
             mm(m, t0, "w", "dy", 1)
-        prep([("v", g, 0, M, 272) for g in range(2)])
+        prep([("v", 0, 0, HALF, 144)])
+        held = interleave("v", 0, HALF, HALF, 144, "held")
         prep([("e", 0, c, HALF, 136) for c in quarters])
-        for m, t0 in early:
+        for m, t0 in early[0:4]:
             mm(m, t0, "v", "e", 0)
-        prep([("e", 1, c, HALF, 136) for c in quarters])
+        job = interleave("e", 1, 0, HALF, 160)
+        quantise(held)
+        for m, t0 in early[4:8]:
+            mm(m, t0, "v", "e", 0)
+        for c in quarters[1:]:
+            last, job = job, interleave("e", 1, c, HALF, 128)
+            quantise(last)
+        for part in (("v", 1, 0, P, 64), ("v", 1, P, P, 64), ("v", 1, HALF, HALF, 128)):
+            last, job = job, interleave(*part)
+            quantise(last)
+        quantise(job)
         for m, t0 in early:
             mm(m, t0, "v", "e", 1, stop=True)
 
-        late = [(0, EARLY, HALF), (0, EARLY + HALF, HALF), (1, EARLY, CHUNK), (2, EARLY, CHUNK), (3, EARLY, CHUNK)]
-        prep([("dy", 0, c, HALF, HALF) for c in halves])
+        late = [(0, EARLY, HALF, 0), (0, EARLY + HALF, P, 1), (0, EARLY + HALF + P, P, 2), (1, EARLY, CHUNK, 3), (2, EARLY, CHUNK, 4), (3, EARLY, CHUNK, 5)]
+        prep([("dy", 1, c, HALF, HALF) for c in halves])
         for m, t0 in early[0:4]:
             drain(on_s, m, t0)
-        prep([("dy", 1, c, HALF, HALF) for c in halves])
-        for m, t0 in early[4:8]:
+        store(0, 2, 0, EARLY)
+        drain(on_v, 2, 0)
+        prep([("e", 0, c, HALF, HALF) for c in halves])
+        for m, t0 in early[5:8]:
             drain(on_s, m, t0)
-        for bank, (m, t0, n) in enumerate(late):
+        store(2, 4, 0, EARLY)
+        for m, t0, n, bank in late:
             open_sum(m, t0, bank)
             mm(m, t0, "w", "dy", 0, start=True, n=n)
-        for m, t0, n in late:
             mm(m, t0, "w", "dy", 1, n=n)
-        store(0, 2, 0, EARLY)
-        store(2, 4, 0, EARLY)
-        prep([("e", 0, EARLY, HALF, HALF), ("e", 0, EARLY + HALF, HALF, 96)])
-        for m, t0, n in late:
+        for m, t0, n, bank in late:
             mm(m, t0, "v", "e", 0, n=n)
-        prep([("e", 1, EARLY, P, 84), ("e", 1, EARLY + P, P, 64)])
+        jobs = [interleave("e", 1, EARLY + c, P, share) for c, share in ((0, 84), (P, 64), (HALF, 80))]
+        quantise(jobs[0])
+        jobs.append(interleave("e", 1, EARLY + HALF + P, P, 80))
+        for job in jobs[1:]:
+            quantise(job)
         mm(0, EARLY, "v", "e", 1, stop=True, n=HALF)
-        for m in (1, 2, 3):
-            mm(m, EARLY, "v", "e", 1, n=HALF)
-        prep([("e", 1, EARLY + HALF, P, 84), ("e", 1, EARLY + HALF + P, P, 64)])
+        mm(1, EARLY, "v", "e", 1, n=HALF)
+        mm(0, EARLY + HALF, "v", "e", 1, stop=True, n=P)
+        mm(0, EARLY + HALF + P, "v", "e", 1, stop=True, n=P)
+        mm(1, EARLY, "v", "e", 1, stop=True, n0=HALF, n=HALF)
+        for m in (2, 3):
+            mm(m, EARLY, "v", "e", 1, stop=True)
         drain(on_s, 0, EARLY, HALF)
-        mm(0, EARLY + HALF, "v", "e", 1, stop=True, n=HALF)
-        for m in (1, 2, 3):
-            mm(m, EARLY, "v", "e", 1, stop=True, n0=HALF, n=HALF)
-        drain(on_v, 0, EARLY + HALF, HALF)
+        drain(on_v, 0, EARLY + HALF, P)
+        drain(on_v, 0, EARLY + HALF + P, P)
         store(0, 1, EARLY, T)
         drain(on_s, 1, EARLY)
         store(1, 2, EARLY, T)

@@ -55,7 +55,7 @@ def tile_mix_aux_fm_none_kernel(tc, w, dy, v, e, out):
         raw = {}
 
         def load_both(name):
-            t = raw_tile(name, 2 * J, M)
+            t = raw_tile(name, 2 * J, hbm[name].shape[1])
             nc.sync.dma_start(out=runs_of(t, 2), in_=hbm[name][:, :].rearrange("(g p j) c -> p g (j c)", g=2, j=J))
             for g in range(2):
                 raw[name, g, 0] = (t[:, g * J : (g + 1) * J, :], 0)
@@ -65,14 +65,12 @@ def tile_mix_aux_fm_none_kernel(tc, w, dy, v, e, out):
             load(t, name, g, J, lo, hi)
             raw[name, g, lo] = (t, lo)
 
-        load_cols("dy", 0, 0, T)
-        load_both("w")
-        load_cols("dy", 1, 0, EARLY)
-        load_cols("v", 0, 0, M)
+        load_both("dy")
         load_cols("e", 0, 0, EARLY)
+        load_both("w")
         load_cols("e", 1, 0, EARLY)
+        load_cols("v", 0, 0, M)
         load_cols("v", 1, 0, M)
-        load_cols("dy", 1, EARLY, T)
         load_cols("e", 0, EARLY, T)
         load_cols("e", 1, EARLY, T)
 
@@ -131,70 +129,91 @@ def tile_mix_aux_fm_none_kernel(tc, w, dy, v, e, out):
 
         on_v, on_s = nc.vector.tensor_copy, nc.scalar.copy
 
-        early = [(m, t0) for m in range(4) for t0 in (0, CHUNK)]
         halves = (EARLY, EARLY + HALF)
-        quarters = range(0, EARLY, HALF)
-        prep([("dy", 0, c, CHUNK, 272) for c in range(0, T, CHUNK)])
-        prep([("w", g, 0, M, 272) for g in range(2)])
-        for bank, (m, t0) in enumerate(early):
-            open_sum(m, t0, bank)
-            mm(m, t0, "w", "dy", 0, start=True)
-        prep([("dy", 1, c, CHUNK, 272) for c in (0, CHUNK)])
-        for m, t0 in early:
-            mm(m, t0, "w", "dy", 1)
-        prep([("v", 0, 0, HALF, 144)])
-        held = interleave("v", 0, HALF, HALF, 144, "held")
-        prep([("e", 0, c, HALF, 136) for c in quarters])
-        for m, t0 in early[0:4]:
-            mm(m, t0, "v", "e", 0)
-        job = interleave("e", 1, 0, HALF, 160)
-        quantise(held)
-        for m, t0 in early[4:8]:
-            mm(m, t0, "v", "e", 0)
-        for c in quarters[1:]:
-            last, job = job, interleave("e", 1, c, HALF, 128)
-            quantise(last)
-        for part in (("v", 1, 0, P, 64), ("v", 1, P, P, 64), ("v", 1, HALF, HALF, 128)):
-            last, job = job, interleave(*part)
-            quantise(last)
-        quantise(job)
-        for m, t0 in early:
-            mm(m, t0, "v", "e", 1, stop=True)
+        quarter = EARLY + HALF + P
+        prep([("dy", g, c, CHUNK, 256) for g in range(2) for c in range(0, T, CHUNK)] + [("e", 0, 0, CHUNK, 272)])
+        prep([("w", g, c, HALF, 136) for c in (0, HALF) for g in range(2)] + [("e", 0, CHUNK, CHUNK, 272)])
+        for m in range(4):
+            for h, t0 in enumerate((0, CHUNK)):
+                open_sum(m, t0, 2 * m + h)
+                mm(m, t0, "w", "dy", 0, start=True)
+                mm(m, t0, "w", "dy", 1)
 
-        late = [(0, EARLY, HALF, 0), (0, EARLY + HALF, P, 1), (0, EARLY + HALF + P, P, 2), (1, EARLY, CHUNK, 3), (2, EARLY, CHUNK, 4), (3, EARLY, CHUNK, 5)]
-        prep([("dy", 1, c, HALF, HALF) for c in halves])
-        for m, t0 in early[0:4]:
-            drain(on_s, m, t0)
-        store(0, 2, 0, EARLY)
-        drain(on_v, 2, 0)
+        a = interleave("e", 1, 0, HALF, 192)
+        b = interleave("e", 1, HALF, HALF, 128)
+        quantise(a)
+        c = interleave("e", 1, CHUNK, HALF, 128)
+        quantise(b)
+        d = interleave("e", 1, CHUNK + HALF, HALF, 128)
+        quantise(c)
+        a = interleave("v", 0, 0, P, 84)
+        b = interleave("v", 0, P, P, 64)
+        quantise(a)
+        c = interleave("v", 0, HALF, HALF, 112)
+        quantise(b)
+        quantise(d)
+        quantise(c)
+        for m in range(4):
+            for t0 in (0, CHUNK):
+                mm(m, t0, "v", "e", 0)
+        a = interleave("v", 1, 0, P, 84)
+        b = interleave("v", 1, P, P, 64)
+        quantise(a)
+        c = interleave("v", 1, HALF, HALF, 128)
+        quantise(b)
+        quantise(c)
+        for m in range(4):
+            for t0 in (0, CHUNK):
+                mm(m, t0, "v", "e", 1, stop=True)
+
+        drain(on_s, 0, 0)
+        drain(on_v, 0, CHUNK)
+        store(0, 1, 0, EARLY)
+        for m in (1, 2):
+            drain(on_s, m, 0)
+            drain(on_s, m, CHUNK)
+            store(m, m + 1, 0, EARLY)
         prep([("e", 0, c, HALF, HALF) for c in halves])
-        for m, t0 in early[5:8]:
-            drain(on_s, m, t0)
-        store(2, 4, 0, EARLY)
-        for m, t0, n, bank in late:
+        late = [(0, EARLY, HALF), (0, EARLY + HALF, P), (0, quarter, P), (1, EARLY, CHUNK), (2, EARLY, CHUNK)]
+        for bank, (m, t0, n) in enumerate(late):
             open_sum(m, t0, bank)
             mm(m, t0, "w", "dy", 0, start=True, n=n)
             mm(m, t0, "w", "dy", 1, n=n)
-        for m, t0, n, bank in late:
+        for m, t0, n in late:
             mm(m, t0, "v", "e", 0, n=n)
-        jobs = [interleave("e", 1, EARLY + c, P, share) for c, share in ((0, 84), (P, 64), (HALF, 80))]
+        drain(on_s, 3, 0)
+        drain(on_s, 3, CHUNK)
+        store(3, 4, 0, EARLY)
+        jobs = [interleave("e", 1, EARLY + c, P, share) for c, share in ((0, P), (P, P))]
         quantise(jobs[0])
-        jobs.append(interleave("e", 1, EARLY + HALF + P, P, 80))
-        for job in jobs[1:]:
-            quantise(job)
+        jobs.append(interleave("e", 1, EARLY + HALF, P, P))
+        quantise(jobs[1])
+        jobs.append(interleave("e", 1, quarter, P, 64))
+        quantise(jobs[2])
+        quantise(jobs[3])
+        for h, t0 in enumerate(halves):
+            open_sum(3, t0, 5 + h)
         mm(0, EARLY, "v", "e", 1, stop=True, n=HALF)
-        mm(1, EARLY, "v", "e", 1, n=HALF)
+        mm(3, EARLY, "w", "dy", 0, start=True, n=HALF)
         mm(0, EARLY + HALF, "v", "e", 1, stop=True, n=P)
-        mm(0, EARLY + HALF + P, "v", "e", 1, stop=True, n=P)
-        mm(1, EARLY, "v", "e", 1, stop=True, n0=HALF, n=HALF)
-        for m in (2, 3):
+        mm(3, EARLY, "w", "dy", 1, n=HALF)
+        mm(0, quarter, "v", "e", 1, stop=True, n=P)
+        for m in (1, 2):
             mm(m, EARLY, "v", "e", 1, stop=True)
+        mm(3, EARLY, "v", "e", 0, n=HALF)
+        mm(3, EARLY, "v", "e", 1, stop=True, n=HALF)
+        mm(3, EARLY + HALF, "w", "dy", 0, start=True, n=HALF)
+        mm(3, EARLY + HALF, "w", "dy", 1, n=HALF)
+        mm(3, EARLY + HALF, "v", "e", 0, n=HALF)
+        mm(3, EARLY + HALF, "v", "e", 1, stop=True, n=HALF)
         drain(on_s, 0, EARLY, HALF)
         drain(on_v, 0, EARLY + HALF, P)
-        drain(on_v, 0, EARLY + HALF + P, P)
+        drain(on_v, 0, quarter, P)
         store(0, 1, EARLY, T)
         drain(on_s, 1, EARLY)
         store(1, 2, EARLY, T)
         drain(on_v, 2, EARLY)
-        drain(on_s, 3, EARLY)
-        store(2, 4, EARLY, T)
+        store(2, 3, EARLY, T)
+        drain(on_s, 3, EARLY, HALF)
+        drain(on_v, 3, EARLY + HALF, HALF)
+        store(3, 4, EARLY, T)

@@ -40,180 +40,149 @@ def tile_mix_aux_fm_none_kernel(tc, w, dy, v, e, out):
                 scales[name, g] = keep.tile([P, width], U8, name="scales_%s%d" % (name, g), align_bytes=64)
         res = keep.tile([P, M // P, T], F32, name="res", align_bytes=DMA_ALIGN)
 
-        def raw_tile(label, rows, cols):
-            t = keep.tile([P, rows * cols], F32, name="raw_" + label, align_bytes=DMA_ALIGN)
-            return t[:].rearrange("p (j c) -> p j c", j=rows)
-
-        def load(dst, name, g, runs, lo, hi):
-            rows = hbm[name][g * K_PASS : (g + 1) * K_PASS, :]
-            src = rows.rearrange("(p r j) c -> p r (j c)", p=P, r=runs)
-            nc.sync.dma_start(out=dst, in_=src[:, :, lo:hi])
-
-        def runs_of(t, runs):
-            return t.rearrange("p (r j) c -> p r (j c)", r=runs)
-
         raw = {}
 
         def load_both(name):
-            t = raw_tile(name, 2 * J, hbm[name].shape[1])
-            nc.sync.dma_start(out=runs_of(t, 2), in_=hbm[name][:, :].rearrange("(g p j) c -> p g (j c)", g=2, j=J))
+            width = hbm[name].shape[1]
+            t = keep.tile([P, 2, J * width], F32, name="raw_%s" % name, align_bytes=DMA_ALIGN)
+            nc.sync.dma_start(out=t[:], in_=hbm[name][:, :].rearrange("(g p j) c -> p g (j c)", g=2, j=J))
             for g in range(2):
-                raw[name, g, 0] = (t[:, g * J : (g + 1) * J, :], 0)
+                for c in range(0, width, P):
+                    raw[name, g, c] = t[:, g, :].rearrange("p (j c) -> p j c", j=J), 0
 
-        def load_cols(name, g, lo, hi):
-            t = raw_tile("%s%d_%d" % (name, g, lo), J, hi - lo)
-            load(t, name, g, J, lo, hi)
-            raw[name, g, lo] = (t, lo)
+        def load(name, g, first, end):
+            t = keep.tile([P, J, end - first], F32, name="raw_%s%d_%d" % (name, g, first), align_bytes=DMA_ALIGN)
+            rows = hbm[name][g * K_PASS : (g + 1) * K_PASS, first:end]
+            nc.sync.dma_start(out=t[:], in_=rows.rearrange("(p j) c -> p j c", j=J))
+            for c in range(first, end, P):
+                raw[name, g, c] = t, first
 
         load_both("dy")
-        load_cols("e", 0, 0, EARLY)
+        load("e", 0, 0, EARLY)
         load_both("w")
-        load_cols("e", 1, 0, EARLY)
-        load_cols("v", 0, 0, M)
-        load_cols("v", 1, 0, M)
-        load_cols("e", 0, EARLY, T)
-        load_cols("e", 1, EARLY, T)
+        load("e", 1, 0, EARLY)
+        load("v", 0, 0, M)
+        load("v", 1, 0, M)
+        load("e", 0, EARLY, T)
+        load("e", 1, EARLY, T)
 
-        def interleave(name, g, c0, cols, v_cols, tag="grouped"):
-            b = stage.tile([P, cols, J], BF16, name=tag, align_bytes=64)
-            t, first = raw[name, g, max(c for (n, h, c) in raw if (n, h) == (name, g) and c <= c0)]
-            for copy, lo, hi in ((nc.vector.tensor_copy, 0, v_cols), (nc.scalar.copy, v_cols, cols)):
+        def interleave(name, g, c0, cols, quarters_on_vector=2):
+            grouped = stage.tile([P, cols, J], BF16, name="grouped", align_bytes=64)
+            t, first = raw[name, g, c0]
+            split = cols * quarters_on_vector // 4
+            for copy, lo, hi in ((nc.vector.tensor_copy, 0, split), (nc.scalar.copy, split, cols)):
                 if hi > lo:
                     copy(
-                        out=b[:, lo:hi, :].rearrange("p (c i) j -> p c j i", i=4),
+                        out=grouped[:, lo:hi, :].rearrange("p (c i) j -> p c j i", i=4),
                         in_=t[:, :, c0 - first + lo : c0 - first + hi].rearrange("p j (c i) -> p c j i", i=4),
                     )
-            return (name, g, c0, cols, b)
+            return name, g, c0, cols, grouped
 
-        def quantise(job):
-            name, g, c0, cols, b = job
+        def quantise(part):
+            name, g, c0, cols, grouped = part
             nc.vector.quantize_mx(
                 out=codes[name, g][:, c0 : c0 + cols].bitcast(fmt[name]),
                 scales=scales[name, g][:, c0 : c0 + cols],
-                in_=b[:].rearrange("p c j -> p (c j)"),
+                in_=grouped[:].rearrange("p c j -> p (c j)"),
             )
 
-        def prep(parts):
+        def prepare(parts):
             last = None
-            for part in parts:
-                job = interleave(*part)
+            for args in parts:
+                part = interleave(*args)
                 if last is not None:
                     quantise(last)
-                last = job
+                last = part
             quantise(last)
 
         acc = {}
 
-        def open_sum(m, t0, bank):
-            acc[m, t0] = psum.tile([P, CHUNK], F32, name="bank%d" % bank)
+        def open_sum(m, t0, n, bank):
+            acc[m, t0] = psum.tile([P, CHUNK], F32, name="bank%d" % bank), n
 
-        def mm(m, t0, sta, mov, g, start=False, stop=False, n0=0, n=CHUNK):
-            rows = slice(m * P, (m + 1) * P)
-            cols = slice(t0 + n0, t0 + n0 + n)
+        def mm(m, t0, sta, mov, g):
+            bank, n = acc[m, t0]
+            rows, cols = slice(m * P, (m + 1) * P), slice(t0, t0 + n)
             nc.tensor.matmul_mx(
-                out=acc[m, t0][:, n0 : n0 + n],
+                out=bank[:, 0:n],
                 lhsT=codes[sta, g][:, rows].bitcast(fmt[sta]),
                 lhsT_scale=scales[sta, g][:, rows],
                 rhs=codes[mov, g][:, cols].bitcast(fmt[mov]),
                 rhs_scale=scales[mov, g][:, cols],
-                start=start,
-                stop=stop,
+                start=(sta, g) == ("w", 0),
+                stop=(sta, g) == ("v", 1),
             )
 
-        def drain(copy, m, t0, n=CHUNK):
-            copy(out=res[:, m, t0 : t0 + n], in_=acc[m, t0][:, 0:n])
+        def drain(copy, m, t0):
+            bank, n = acc[m, t0]
+            copy(out=res[:, m, t0 : t0 + n], in_=bank[:, 0:n])
 
         def store(m0, m1, t0, t1):
             rows = out[m0 * P : m1 * P, t0:t1]
             nc.sync.dma_start(out=rows.rearrange("(m p) t -> p m t", p=P), in_=res[:, m0:m1, t0:t1])
 
-        on_v, on_s = nc.vector.tensor_copy, nc.scalar.copy
+        on_vector, on_scalar = nc.vector.tensor_copy, nc.scalar.copy
 
-        halves = (EARLY, EARLY + HALF)
-        quarter = EARLY + HALF + P
-        prep([("dy", g, c, CHUNK, 256) for g in range(2) for c in range(0, T, CHUNK)] + [("e", 0, 0, CHUNK, 272)])
-        prep([("w", g, c, HALF, 136) for c in (0, HALF) for g in range(2)] + [("e", 0, CHUNK, CHUNK, 272)])
-        for m in range(4):
-            for h, t0 in enumerate((0, CHUNK)):
-                open_sum(m, t0, 2 * m + h)
-                mm(m, t0, "w", "dy", 0, start=True)
-                mm(m, t0, "w", "dy", 1)
+        early = [(m, t0) for m in range(M // P) for t0 in (0, CHUNK)]
+        prepare([("dy", g, c, CHUNK) for g in range(2) for c in range(0, T, CHUNK)] + [("e", 0, 0, CHUNK)])
+        prepare([("w", g, c, HALF) for c in (0, HALF) for g in range(2)] + [("e", 0, CHUNK, CHUNK)])
+        for bank, (m, t0) in enumerate(early):
+            open_sum(m, t0, CHUNK, bank)
+            mm(m, t0, "w", "dy", 0)
+            mm(m, t0, "w", "dy", 1)
 
-        a = interleave("e", 1, 0, HALF, 192)
-        b = interleave("e", 1, HALF, HALF, 128)
-        quantise(a)
-        c = interleave("e", 1, CHUNK, HALF, 128)
-        quantise(b)
-        d = interleave("e", 1, CHUNK + HALF, HALF, 128)
-        quantise(c)
-        a = interleave("v", 0, 0, P, 84)
-        b = interleave("v", 0, P, P, 64)
-        quantise(a)
-        c = interleave("v", 0, HALF, HALF, 112)
-        quantise(b)
-        quantise(d)
-        quantise(c)
-        for m in range(4):
-            for t0 in (0, CHUNK):
-                mm(m, t0, "v", "e", 0)
-        a = interleave("v", 1, 0, P, 84)
-        b = interleave("v", 1, P, P, 64)
-        quantise(a)
-        c = interleave("v", 1, HALF, HALF, 128)
-        quantise(b)
-        quantise(c)
-        for m in range(4):
-            for t0 in (0, CHUNK):
-                mm(m, t0, "v", "e", 1, stop=True)
+        prepare([("e", 1, 0, HALF, 3), ("e", 1, HALF, HALF), ("e", 1, CHUNK, HALF)])
+        prepare([("v", 0, 0, P, 3), ("v", 0, P, P), ("v", 0, HALF, HALF), ("e", 1, CHUNK + HALF, HALF)])
+        for m, t0 in early:
+            mm(m, t0, "v", "e", 0)
+        prepare([("v", 1, 0, P, 3), ("v", 1, P, P), ("v", 1, HALF, HALF)])
+        for m, t0 in early:
+            mm(m, t0, "v", "e", 1)
 
-        drain(on_s, 0, 0)
-        drain(on_v, 0, CHUNK)
+        drain(on_scalar, 0, 0)
+        drain(on_vector, 0, CHUNK)
         store(0, 1, 0, EARLY)
-        for m in (1, 2):
-            drain(on_s, m, 0)
-            drain(on_s, m, CHUNK)
-            store(m, m + 1, 0, EARLY)
-        prep([("e", 0, c, HALF, HALF) for c in halves])
-        late = [(0, EARLY, HALF), (0, EARLY + HALF, P), (0, quarter, P), (1, EARLY, CHUNK), (2, EARLY, CHUNK)]
-        for bank, (m, t0, n) in enumerate(late):
-            open_sum(m, t0, bank)
-            mm(m, t0, "w", "dy", 0, start=True, n=n)
-            mm(m, t0, "w", "dy", 1, n=n)
+        for m, t0 in early[2:4]:
+            drain(on_scalar, m, t0)
+        store(1, 2, 0, EARLY)
+        prepare([("e", 0, c, HALF, 4) for c in (EARLY, EARLY + HALF)])
+        for m, t0 in early[4:7]:
+            drain(on_scalar, m, t0)
+        drain(on_vector, 3, CHUNK)
+        store(2, 4, 0, EARLY)
+
+        mid, last = EARLY + HALF, T - P
+        late = [(0, EARLY, HALF), (1, EARLY, HALF), (0, mid, P), (0, last, P), (1, mid, HALF), (2, EARLY, CHUNK)]
+        for group in (late[0:5], late[5:6]):
+            for m, t0, n in group:
+                open_sum(m, t0, n, late.index((m, t0, n)))
+                mm(m, t0, "w", "dy", 0)
+                mm(m, t0, "w", "dy", 1)
+            for m, t0, n in group:
+                mm(m, t0, "v", "e", 0)
+        parts = [interleave("e", 1, EARLY, P, 4), interleave("e", 1, EARLY + P, P), interleave("e", 1, mid, P)]
+        quantise(parts[0])
+        parts.append(interleave("e", 1, last, P))
+        for part in parts[1:]:
+            quantise(part)
         for m, t0, n in late:
-            mm(m, t0, "v", "e", 0, n=n)
-        drain(on_s, 3, 0)
-        drain(on_s, 3, CHUNK)
-        store(3, 4, 0, EARLY)
-        jobs = [interleave("e", 1, EARLY + c, P, share) for c, share in ((0, P), (P, P))]
-        quantise(jobs[0])
-        jobs.append(interleave("e", 1, EARLY + HALF, P, P))
-        quantise(jobs[1])
-        jobs.append(interleave("e", 1, quarter, P, 64))
-        quantise(jobs[2])
-        quantise(jobs[3])
-        for h, t0 in enumerate(halves):
-            open_sum(3, t0, 5 + h)
-        mm(0, EARLY, "v", "e", 1, stop=True, n=HALF)
-        mm(3, EARLY, "w", "dy", 0, start=True, n=HALF)
-        mm(0, EARLY + HALF, "v", "e", 1, stop=True, n=P)
-        mm(3, EARLY, "w", "dy", 1, n=HALF)
-        mm(0, quarter, "v", "e", 1, stop=True, n=P)
-        for m in (1, 2):
-            mm(m, EARLY, "v", "e", 1, stop=True)
-        mm(3, EARLY, "v", "e", 0, n=HALF)
-        mm(3, EARLY, "v", "e", 1, stop=True, n=HALF)
-        mm(3, EARLY + HALF, "w", "dy", 0, start=True, n=HALF)
-        mm(3, EARLY + HALF, "w", "dy", 1, n=HALF)
-        mm(3, EARLY + HALF, "v", "e", 0, n=HALF)
-        mm(3, EARLY + HALF, "v", "e", 1, stop=True, n=HALF)
-        drain(on_s, 0, EARLY, HALF)
-        drain(on_v, 0, EARLY + HALF, P)
-        drain(on_v, 0, quarter, P)
+            mm(m, t0, "v", "e", 1)
+        for h, t0 in enumerate((EARLY, mid)):
+            open_sum(3, t0, HALF, len(late) + h)
+            mm(3, t0, "w", "dy", 0)
+            mm(3, t0, "w", "dy", 1)
+            mm(3, t0, "v", "e", 0)
+            mm(3, t0, "v", "e", 1)
+
+        drain(on_scalar, 0, EARLY)
+        drain(on_vector, 0, mid)
+        drain(on_vector, 0, last)
         store(0, 1, EARLY, T)
-        drain(on_s, 1, EARLY)
+        drain(on_scalar, 1, EARLY)
+        drain(on_scalar, 1, mid)
         store(1, 2, EARLY, T)
-        drain(on_v, 2, EARLY)
+        drain(on_vector, 2, EARLY)
         store(2, 3, EARLY, T)
-        drain(on_s, 3, EARLY, HALF)
-        drain(on_v, 3, EARLY + HALF, HALF)
+        drain(on_scalar, 3, EARLY)
+        drain(on_vector, 3, mid)
         store(3, 4, EARLY, T)

@@ -160,6 +160,8 @@ def tile_mix_aux_fm_none_kernel(tc, w, dy, v, e, out):
                 mm(m, t0, "w", "dy", 1)
             for m, t0, n in group:
                 mm(m, t0, "v", "e", 0)
+        open_sum(3, EARLY, CHUNK, len(late))
+        mm(3, EARLY, "w", "dy", 0)
         parts = [interleave("e", 1, EARLY, P, 4), interleave("e", 1, EARLY + P, P), interleave("e", 1, mid, P)]
         quantise(parts[0])
         parts.append(interleave("e", 1, last, P))
@@ -167,12 +169,9 @@ def tile_mix_aux_fm_none_kernel(tc, w, dy, v, e, out):
             quantise(part)
         for m, t0, n in late:
             mm(m, t0, "v", "e", 1)
-        for h, t0 in enumerate((EARLY, mid)):
-            open_sum(3, t0, HALF, len(late) + h)
-            mm(3, t0, "w", "dy", 0)
-            mm(3, t0, "w", "dy", 1)
-            mm(3, t0, "v", "e", 0)
-            mm(3, t0, "v", "e", 1)
+        mm(3, EARLY, "w", "dy", 1)
+        mm(3, EARLY, "v", "e", 0)
+        mm(3, EARLY, "v", "e", 1)
 
         drain(on_scalar, 0, EARLY)
         drain(on_vector, 0, mid)
@@ -184,5 +183,4 @@ def tile_mix_aux_fm_none_kernel(tc, w, dy, v, e, out):
         drain(on_vector, 2, EARLY)
         store(2, 3, EARLY, T)
         drain(on_scalar, 3, EARLY)
-        drain(on_vector, 3, mid)
         store(3, 4, EARLY, T)

@@ -18,7 +18,7 @@ K_PASS = P * J
 CHUNK = 512
 HALF = 256
 EARLY = 1024
-DMA_ALIGN = 256
+DMA_ALIGN = 2048
 
 
 def tile_mix_aux_fm_none_kernel(tc, w, dy, v, e, out):

@@ -18,169 +18,192 @@ K_PASS = P * J
 CHUNK = 512
 HALF = 256
 EARLY = 1024
-DMA_ALIGN = 2048
+DMA_ALIGN = 256
 
 
 def tile_mix_aux_fm_none_kernel(tc, w, dy, v, e, out):
     nc = tc.nc
     hbm = {"w": w, "dy": dy, "v": v, "e": e}
     fmt = {"w": E4M3, "dy": E5M2, "v": E4M3, "e": E4M3}
+    on_vector, on_scalar = nc.vector.tensor_copy, nc.scalar.copy
 
     with ExitStack() as ctx:
         keep = ctx.enter_context(tc.tile_pool(name="keep", bufs=1))
-        stage = ctx.enter_context(tc.tile_pool(name="stage", bufs=5))
         psum = ctx.enter_context(tc.psum_pool(name="psum", bufs=1))
         ctx.enter_context(tc.manual_schedule())
 
-        codes, scales = {}, {}
-        for name in ("dy", "e", "w", "v"):
-            width = hbm[name].shape[1]
-            for g in range(2):
-                codes[name, g] = keep.tile([P, width], U32, name="codes_%s%d" % (name, g), align_bytes=64)
-                scales[name, g] = keep.tile([P, width], U8, name="scales_%s%d" % (name, g), align_bytes=64)
-        res = keep.tile([P, M // P, T], F32, name="res", align_bytes=DMA_ALIGN)
+        width = {name: hbm[name].shape[1] for name in hbm}
+        codes = {name: keep.tile([P, 2 * width[name]], U32, name="codes_" + name, align_bytes=64) for name in hbm}
+        scales = {name: keep.tile([P, 2 * width[name]], U8, name="scales_" + name, align_bytes=64) for name in hbm}
 
-        raw = {}
-
-        def load_both(name):
-            width = hbm[name].shape[1]
-            t = keep.tile([P, 2, J * width], F32, name="raw_%s" % name, align_bytes=DMA_ALIGN)
-            nc.sync.dma_start(out=t[:], in_=hbm[name][:, :].rearrange("(g p j) c -> p g (j c)", g=2, j=J))
-            for g in range(2):
-                for c in range(0, width, P):
-                    raw[name, g, c] = t[:, g, :].rearrange("p (j c) -> p j c", j=J), 0
+        raw, staged = {}, {}
 
         def load(name, g, first, end):
             t = keep.tile([P, J, end - first], F32, name="raw_%s%d_%d" % (name, g, first), align_bytes=DMA_ALIGN)
             rows = hbm[name][g * K_PASS : (g + 1) * K_PASS, first:end]
             nc.sync.dma_start(out=t[:], in_=rows.rearrange("(p j) c -> p j c", j=J))
-            for c in range(first, end, P):
+            for c in range(first, end, 64):
                 raw[name, g, c] = t, first
 
-        load_both("dy")
-        load("e", 0, 0, EARLY)
+        def load_both(name):
+            t = keep.tile([P, 2, J * width[name]], F32, name="raw_" + name, align_bytes=DMA_ALIGN)
+            nc.sync.dma_start(out=t[:], in_=hbm[name][:, :].rearrange("(g p j) c -> p g (j c)", g=2, j=J))
+            raw[name] = t
+            for g in range(2):
+                for c in range(0, width[name], 64):
+                    raw[name, g, c] = t[:, g, :].rearrange("p (j c) -> p j c", j=J), 0
+
+        def stage(name, first, end):
+            t = keep.tile([P, J * (end - first)], BF16, name="staged_%s%d" % (name, first), align_bytes=64)
+            for word in range(first, end, 64):
+                staged[name, word] = t, first
+
+        def interleave(copy, name, g, first, end):
+            src, src0 = raw[name, g, first]
+            word = g * width[name] + first
+            dst, dst0 = staged[name, word]
+            lo = J * (word - dst0)
+            copy(
+                out=dst[:, lo : lo + J * (end - first)].rearrange("p (c i j) -> p c j i", i=4, j=J),
+                in_=src[:, :, first - src0 : end - src0].rearrange("p j (c i) -> p c j i", i=4),
+            )
+
+        def interleave_both(copy, name):
+            copy(
+                out=staged[name, 0][0][:].rearrange("p (g c i j) -> p g c j i", g=2, i=4, j=J),
+                in_=raw[name][:].rearrange("p g (j c i) -> p g c j i", j=J, i=4),
+            )
+
+        def quantise(name, first, end):
+            src, src0 = staged[name, first]
+            nc.vector.quantize_mx(
+                out=codes[name][:, first:end].bitcast(fmt[name]),
+                scales=scales[name][:, first:end],
+                in_=src[:, J * (first - src0) : J * (end - src0)],
+            )
+
+        acc, done, total = {}, {}, {}
+
+        def open_sum(m, t0, bank, n=CHUNK, passes=4):
+            acc[m, t0] = psum.tile([P, CHUNK], F32, name="bank%d" % bank)[:, 0:n]
+            done[m, t0], total[m, t0] = 0, passes
+
+        def mm(m, t0, sta, mov, g, lo=0, hi=None):
+            hi = hi or acc[m, t0].shape[1]
+            rows = slice(g * M + m * P, g * M + (m + 1) * P)
+            cols = slice(g * T + t0 + lo, g * T + t0 + hi)
+            nc.tensor.matmul_mx(
+                out=acc[m, t0][:, lo:hi],
+                lhsT=codes[sta][:, rows].bitcast(fmt[sta]),
+                lhsT_scale=scales[sta][:, rows],
+                rhs=codes[mov][:, cols].bitcast(fmt[mov]),
+                rhs_scale=scales[mov][:, cols],
+                start=done[m, t0] == 0,
+                stop=done[m, t0] == total[m, t0] - 1,
+            )
+            done[m, t0] += 1
+
+        def drain(copy, m, t0, lo=0, hi=None):
+            hi = hi or acc[m, t0].shape[1]
+            copy(out=res[:, m, t0 + lo : t0 + hi], in_=acc[m, t0][:, lo:hi])
+
+        def store(m0, m1, t0, t1):
+            rows = out[m0 * P : m1 * P, t0:t1]
+            nc.sync.dma_start(out=rows.rearrange("(m p) t -> p m t", p=P), in_=res[:, m0:m1, t0:t1])
+
+        load("dy", 0, 0, T)
+        load("dy", 1, 0, T)
         load_both("w")
+        load("e", 0, 0, EARLY)
         load("e", 1, 0, EARLY)
         load("v", 0, 0, M)
         load("v", 1, 0, M)
         load("e", 0, EARLY, T)
         load("e", 1, EARLY, T)
 
-        def interleave(name, g, c0, cols, quarters_on_vector=2):
-            grouped = stage.tile([P, cols, J], BF16, name="grouped", align_bytes=64)
-            t, first = raw[name, g, c0]
-            split = cols * quarters_on_vector // 4
-            for copy, lo, hi in ((nc.vector.tensor_copy, 0, split), (nc.scalar.copy, split, cols)):
-                if hi > lo:
-                    copy(
-                        out=grouped[:, lo:hi, :].rearrange("p (c i) j -> p c j i", i=4),
-                        in_=t[:, :, c0 - first + lo : c0 - first + hi].rearrange("p j (c i) -> p c j i", i=4),
-                    )
-            return name, g, c0, cols, grouped
+        tiles = range(M // P)
+        early = [(m, t0) for m in tiles for t0 in (0, CHUNK)]
 
-        def quantise(part):
-            name, g, c0, cols, grouped = part
-            nc.vector.quantize_mx(
-                out=codes[name, g][:, c0 : c0 + cols].bitcast(fmt[name]),
-                scales=scales[name, g][:, c0 : c0 + cols],
-                in_=grouped[:].rearrange("p c j -> p (c j)"),
-            )
-
-        def prepare(parts):
-            last = None
-            for args in parts:
-                part = interleave(*args)
-                if last is not None:
-                    quantise(last)
-                last = part
-            quantise(last)
-
-        acc = {}
-
-        def open_sum(m, t0, n, bank):
-            acc[m, t0] = psum.tile([P, CHUNK], F32, name="bank%d" % bank), n
-
-        def mm(m, t0, sta, mov, g):
-            bank, n = acc[m, t0]
-            rows, cols = slice(m * P, (m + 1) * P), slice(t0, t0 + n)
-            nc.tensor.matmul_mx(
-                out=bank[:, 0:n],
-                lhsT=codes[sta, g][:, rows].bitcast(fmt[sta]),
-                lhsT_scale=scales[sta, g][:, rows],
-                rhs=codes[mov, g][:, cols].bitcast(fmt[mov]),
-                rhs_scale=scales[mov, g][:, cols],
-                start=(sta, g) == ("w", 0),
-                stop=(sta, g) == ("v", 1),
-            )
-
-        def drain(copy, m, t0):
-            bank, n = acc[m, t0]
-            copy(out=res[:, m, t0 : t0 + n], in_=bank[:, 0:n])
-
-        def store(m0, m1, t0, t1):
-            rows = out[m0 * P : m1 * P, t0:t1]
-            nc.sync.dma_start(out=rows.rearrange("(m p) t -> p m t", p=P), in_=res[:, m0:m1, t0:t1])
-
-        on_vector, on_scalar = nc.vector.tensor_copy, nc.scalar.copy
-
-        early = [(m, t0) for m in range(M // P) for t0 in (0, CHUNK)]
-        prepare([("dy", g, c, CHUNK) for g in range(2) for c in range(0, T, CHUNK)] + [("e", 0, 0, CHUNK)])
-        prepare([("w", g, c, HALF) for c in (0, HALF) for g in range(2)] + [("e", 0, CHUNK, CHUNK)])
+        stage("dy", 0, T + CHUNK)
+        stage("dy", T + CHUNK, 2 * T)
+        stage("w", 0, 2 * M)
+        interleave(on_scalar, "dy", 0, 0, T)
+        res = keep.tile([P, M // P, T], F32, name="raw_dy0_0", align_bytes=DMA_ALIGN)
+        interleave(on_scalar, "dy", 1, 0, CHUNK)
+        interleave(on_vector, "dy", 1, CHUNK, T)
+        quantise("dy", 0, EARLY)
+        quantise("dy", T + CHUNK, 2 * T)
+        quantise("dy", EARLY, T + CHUNK)
+        interleave_both(on_scalar, "w")
+        quantise("w", 0, 2 * M)
         for bank, (m, t0) in enumerate(early):
-            open_sum(m, t0, CHUNK, bank)
+            open_sum(m, t0, bank)
             mm(m, t0, "w", "dy", 0)
             mm(m, t0, "w", "dy", 1)
 
-        prepare([("e", 1, 0, HALF, 3), ("e", 1, HALF, HALF), ("e", 1, CHUNK, HALF)])
-        prepare([("v", 0, 0, P, 3), ("v", 0, P, P), ("v", 0, HALF, HALF), ("e", 1, CHUNK + HALF, HALF)])
-        for m, t0 in early:
-            mm(m, t0, "v", "e", 0)
-        prepare([("v", 1, 0, P, 3), ("v", 1, P, P), ("v", 1, HALF, HALF)])
-        for m, t0 in early:
-            mm(m, t0, "v", "e", 1)
+        for g in range(2):
+            for c in (0, CHUNK):
+                stage("e", g * T + c, g * T + c + CHUNK)
+            stage("v", g * M, g * M + P)
+            stage("v", g * M + P, (g + 1) * M)
+        interleave(on_vector, "e", 0, 0, CHUNK)
+        interleave(on_scalar, "e", 0, CHUNK, EARLY)
+        quantise("e", CHUNK, EARLY)
+        quantise("e", 0, CHUNK)
+        interleave(on_vector, "e", 1, 0, CHUNK)
+        interleave(on_scalar, "e", 1, CHUNK, EARLY)
+        quantise("e", T, T + CHUNK)
+        for g in range(2):
+            interleave(on_scalar, "v", g, 0, P)
+            interleave(on_vector, "v", g, P, M)
+            quantise("v", g * M, g * M + P)
+            quantise("v", g * M + P, (g + 1) * M)
+            if g == 0:
+                quantise("e", T + CHUNK, T + EARLY)
+            for m, t0 in early:
+                mm(m, t0, "v", "e", g)
 
-        drain(on_scalar, 0, 0)
-        drain(on_vector, 0, CHUNK)
+        mid = EARLY + HALF
+        stage("e", EARLY, T)
+        stage("e", T + EARLY, T + mid)
+        stage("e", T + mid, 2 * T)
+        drain(on_vector, 0, 0)
+        drain(on_scalar, 0, CHUNK)
         store(0, 1, 0, EARLY)
-        for m, t0 in early[2:4]:
-            drain(on_scalar, m, t0)
-        store(1, 2, 0, EARLY)
-        prepare([("e", 0, c, HALF, 4) for c in (EARLY, EARLY + HALF)])
-        for m, t0 in early[4:7]:
-            drain(on_scalar, m, t0)
-        drain(on_vector, 3, CHUNK)
-        store(2, 4, 0, EARLY)
+        interleave(on_vector, "e", 0, EARLY, T)
+        quantise("e", EARLY, T)
+        for m in tiles[1:]:
+            drain(on_scalar, m, 0)
+            drain(on_scalar, m, CHUNK)
+            store(m, m + 1, 0, EARLY)
+        interleave(on_vector, "e", 1, EARLY, mid)
+        interleave(on_vector, "e", 1, mid, T)
+        quantise("e", T + EARLY, T + mid)
+        quantise("e", T + mid, 2 * T)
 
-        mid, last = EARLY + HALF, T - P
-        late = [(0, EARLY, HALF), (1, EARLY, HALF), (0, mid, P), (0, last, P), (1, mid, HALF), (2, EARLY, CHUNK)]
-        for group in (late[0:5], late[5:6]):
-            for m, t0, n in group:
-                open_sum(m, t0, n, late.index((m, t0, n)))
-                mm(m, t0, "w", "dy", 0)
-                mm(m, t0, "w", "dy", 1)
-            for m, t0, n in group:
-                mm(m, t0, "v", "e", 0)
-        open_sum(3, EARLY, CHUNK, len(late))
+        late = [(0, EARLY, HALF, 4), (0, mid, HALF, 4), (1, EARLY, CHUNK, 5), (2, EARLY, CHUNK, 4), (3, EARLY, CHUNK, 4)]
+        for bank, (m, t0, n, passes) in enumerate(late):
+            open_sum(m, t0, bank, n, passes)
+        for m, t0, n, passes in late[0:4]:
+            mm(m, t0, "w", "dy", 0)
+            mm(m, t0, "w", "dy", 1)
+        for m, t0, n, passes in late[0:4]:
+            mm(m, t0, "v", "e", 0)
         mm(3, EARLY, "w", "dy", 0)
-        parts = [interleave("e", 1, EARLY, P, 4), interleave("e", 1, EARLY + P, P), interleave("e", 1, mid, P)]
-        quantise(parts[0])
-        parts.append(interleave("e", 1, last, P))
-        for part in parts[1:]:
-            quantise(part)
-        for m, t0, n in late:
-            mm(m, t0, "v", "e", 1)
+        mm(0, EARLY, "v", "e", 1)
+        mm(1, EARLY, "v", "e", 1, 0, HALF)
+        mm(0, mid, "v", "e", 1)
+        mm(1, EARLY, "v", "e", 1, HALF, CHUNK)
+        mm(2, EARLY, "v", "e", 1)
         mm(3, EARLY, "w", "dy", 1)
         mm(3, EARLY, "v", "e", 0)
         mm(3, EARLY, "v", "e", 1)
 
         drain(on_scalar, 0, EARLY)
         drain(on_vector, 0, mid)
-        drain(on_vector, 0, last)
         store(0, 1, EARLY, T)
         drain(on_scalar, 1, EARLY)
-        drain(on_scalar, 1, mid)
-        store(1, 2, EARLY, T)
         drain(on_vector, 2, EARLY)
-        store(2, 3, EARLY, T)
+        store(1, 3, EARLY, T)
         drain(on_scalar, 3, EARLY)
         store(3, 4, EARLY, T)

@@ -115,18 +115,18 @@ def tile_mix_aux_fm_none_kernel(tc, w, dy, v, e, out):
         load("dy", 1, 0, T)
         load_both("w")
         load("e", 0, 0, EARLY)
-        load("e", 1, 0, EARLY)
-        load("v", 0, 0, M)
-        load("v", 1, 0, M)
+        load_both("v")
+        load("e", 1, 0, CHUNK)
+        load("e", 1, CHUNK, EARLY)
         load("e", 0, EARLY, T)
         load("e", 1, EARLY, T)
 
         tiles = range(M // P)
-        early = [(m, t0) for m in tiles for t0 in (0, CHUNK)]
+        early = [(m, t0) for t0 in (0, CHUNK) for m in tiles]
+        mid = EARLY + HALF
 
         stage("dy", 0, T + CHUNK)
         stage("dy", T + CHUNK, 2 * T)
-        stage("w", 0, 2 * M)
         interleave(on_scalar, "dy", 0, 0, T)
         res = keep.tile([P, M // P, T], F32, name="raw_dy0_0", align_bytes=DMA_ALIGN)
         interleave(on_scalar, "dy", 1, 0, CHUNK)
@@ -134,76 +134,101 @@ def tile_mix_aux_fm_none_kernel(tc, w, dy, v, e, out):
         quantise("dy", 0, EARLY)
         quantise("dy", T + CHUNK, 2 * T)
         quantise("dy", EARLY, T + CHUNK)
-        interleave_both(on_scalar, "w")
-        quantise("w", 0, 2 * M)
+        stage("w", 0, M)
+        stage("w", M, 2 * M)
+        interleave(on_vector, "w", 0, 0, M)
+        interleave(on_scalar, "w", 1, 0, M)
+        quantise("w", M, 2 * M)
+        quantise("w", 0, M)
         for bank, (m, t0) in enumerate(early):
             open_sum(m, t0, bank)
             mm(m, t0, "w", "dy", 0)
             mm(m, t0, "w", "dy", 1)
 
-        for g in range(2):
-            for c in (0, CHUNK):
-                stage("e", g * T + c, g * T + c + CHUNK)
-            stage("v", g * M, g * M + P)
-            stage("v", g * M + P, (g + 1) * M)
+        stage("e", 0, CHUNK)
+        stage("e", CHUNK, EARLY)
         interleave(on_vector, "e", 0, 0, CHUNK)
         interleave(on_scalar, "e", 0, CHUNK, EARLY)
-        quantise("e", CHUNK, EARLY)
         quantise("e", 0, CHUNK)
-        interleave(on_vector, "e", 1, 0, CHUNK)
-        interleave(on_scalar, "e", 1, CHUNK, EARLY)
-        quantise("e", T, T + CHUNK)
-        for g in range(2):
-            interleave(on_scalar, "v", g, 0, P)
-            interleave(on_vector, "v", g, P, M)
-            quantise("v", g * M, g * M + P)
-            quantise("v", g * M + P, (g + 1) * M)
-            if g == 0:
-                quantise("e", T + CHUNK, T + EARLY)
-            for m, t0 in early:
-                mm(m, t0, "v", "e", g)
+        quantise("e", CHUNK, EARLY)
 
-        mid = EARLY + HALF
-        stage("e", EARLY, T)
-        stage("e", T + EARLY, T + mid)
-        stage("e", T + mid, 2 * T)
-        drain(on_vector, 0, 0)
-        drain(on_scalar, 0, CHUNK)
-        store(0, 1, 0, EARLY)
-        interleave(on_vector, "e", 0, EARLY, T)
-        quantise("e", EARLY, T)
-        for m in tiles[1:]:
+        stage("v", 0, P)
+        stage("v", P, M)
+        stage("v", M, M + HALF)
+        stage("v", M + HALF, 2 * M)
+        interleave(on_scalar, "v", 0, 0, P)
+        interleave(on_vector, "v", 0, P, M)
+        interleave(on_scalar, "v", 1, HALF, M)
+        quantise("v", 0, P)
+        interleave(on_vector, "v", 1, 0, HALF)
+        quantise("v", P, M)
+        for m in tiles:
+            for t0 in (0, CHUNK):
+                mm(m, t0, "v", "e", 0)
+
+        for c in range(0, EARLY, HALF):
+            stage("e", T + c, T + c + HALF)
+        interleave(on_scalar, "e", 1, HALF, CHUNK)
+        quantise("v", M, M + HALF)
+        interleave(on_vector, "e", 1, 0, HALF)
+        quantise("v", M + HALF, 2 * M)
+        quantise("e", T, T + HALF)
+        quantise("e", T + HALF, T + CHUNK)
+        for m in tiles:
+            mm(m, 0, "v", "e", 1)
+        for c in (CHUNK, CHUNK + HALF):
+            interleave(on_vector, "e", 1, c, c + HALF)
+        for c in (CHUNK, CHUNK + HALF):
+            quantise("e", T + c, T + c + HALF)
+        for m in tiles:
             drain(on_scalar, m, 0)
-            drain(on_scalar, m, CHUNK)
-            store(m, m + 1, 0, EARLY)
-        interleave(on_vector, "e", 1, EARLY, mid)
-        interleave(on_vector, "e", 1, mid, T)
-        quantise("e", T + EARLY, T + mid)
-        quantise("e", T + mid, 2 * T)
+        store(0, 4, 0, CHUNK)
 
-        late = [(0, EARLY, HALF, 4), (0, mid, HALF, 4), (1, EARLY, CHUNK, 5), (2, EARLY, CHUNK, 4), (3, EARLY, CHUNK, 4)]
-        for bank, (m, t0, n, passes) in enumerate(late):
-            open_sum(m, t0, bank, n, passes)
-        for m, t0, n, passes in late[0:4]:
+        late = [(0, EARLY, HALF), (1, EARLY, HALF), (0, mid, HALF), (1, mid, HALF), (2, EARLY, CHUNK), (3, EARLY, CHUNK)]
+
+        def open_late(i):
+            m, t0, n = late[i]
+            open_sum(m, t0, i, n)
             mm(m, t0, "w", "dy", 0)
             mm(m, t0, "w", "dy", 1)
-        for m, t0, n, passes in late[0:4]:
-            mm(m, t0, "v", "e", 0)
-        mm(3, EARLY, "w", "dy", 0)
-        mm(0, EARLY, "v", "e", 1)
-        mm(1, EARLY, "v", "e", 1, 0, HALF)
-        mm(0, mid, "v", "e", 1)
-        mm(1, EARLY, "v", "e", 1, HALF, CHUNK)
-        mm(2, EARLY, "v", "e", 1)
-        mm(3, EARLY, "w", "dy", 1)
-        mm(3, EARLY, "v", "e", 0)
-        mm(3, EARLY, "v", "e", 1)
 
-        drain(on_scalar, 0, EARLY)
-        drain(on_vector, 0, mid)
-        store(0, 1, EARLY, T)
-        drain(on_scalar, 1, EARLY)
-        drain(on_vector, 2, EARLY)
-        store(1, 3, EARLY, T)
-        drain(on_scalar, 3, EARLY)
-        store(3, 4, EARLY, T)
+        def late_pass(g, first, end):
+            for m, t0, n in late[first:end]:
+                mm(m, t0, "v", "e", g)
+
+        for i in range(2):
+            open_late(i)
+        for m in tiles:
+            mm(m, CHUNK, "v", "e", 1)
+
+        stage("e", EARLY, mid)
+        stage("e", mid, T)
+        for c in range(EARLY, mid, P):
+            stage("e", T + c, T + c + P)
+        for c in range(mid, T, P):
+            stage("e", T + c, T + c + P)
+        for c in (EARLY, mid):
+            interleave(on_vector, "e", 0, c, c + HALF)
+        for m in tiles[0:3]:
+            drain(on_scalar, m, CHUNK)
+        drain(on_vector, 3, CHUNK)
+        store(0, 4, CHUNK, EARLY)
+        for c in (EARLY, mid):
+            quantise("e", c, c + HALF)
+        for i in range(2, 6):
+            open_late(i)
+        late_pass(0, 0, 6)
+        for c in (EARLY, mid):
+            interleave(on_scalar, "e", 1, c, c + P)
+            interleave(on_vector, "e", 1, c + P, c + HALF)
+        for c in (EARLY, EARLY + P, mid + P, mid):
+            quantise("e", T + c, T + c + P)
+        late_pass(1, 0, 6)
+
+        for t0 in (EARLY, mid):
+            drain(on_scalar, 0, t0)
+            drain(on_vector, 1, t0)
+            store(0, 2, t0, t0 + HALF)
+        drain(on_scalar, 2, EARLY)
+        drain(on_vector, 3, EARLY)
+        store(2, 4, EARLY, T)

@@ -180,9 +180,10 @@ def tile_mix_aux_fm_none_kernel(tc, w, dy, v, e, out):
             interleave(on_vector, "e", 1, c, c + HALF)
         for c in (CHUNK, CHUNK + HALF):
             quantise("e", T + c, T + c + HALF)
-        for m in tiles:
+        for m in (0, 2):
             drain(on_scalar, m, 0)
-        store(0, 4, 0, CHUNK)
+            drain(on_scalar, m + 1, 0)
+            store(m, m + 2, 0, CHUNK)
 
         late = [(0, EARLY, HALF), (1, EARLY, HALF), (0, mid, HALF), (1, mid, HALF), (2, EARLY, CHUNK), (3, EARLY, CHUNK)]
 

@@ -107,9 +107,9 @@ def tile_mix_aux_fm_none_kernel(tc, w, dy, v, e, out):
             hi = hi or acc[m, t0].shape[1]
             copy(out=res[:, m, t0 + lo : t0 + hi], in_=acc[m, t0][:, lo:hi])
 
-        def store(m0, m1, t0, t1):
+        def store(m0, m1, t0, t1, queue=nc.sync):
             rows = out[m0 * P : m1 * P, t0:t1]
-            nc.sync.dma_start(out=rows.rearrange("(m p) t -> p m t", p=P), in_=res[:, m0:m1, t0:t1])
+            queue.dma_start(out=rows.rearrange("(m p) t -> p m t", p=P), in_=res[:, m0:m1, t0:t1])
 
         load("dy", 0, 0, T)
         load("dy", 1, 0, T)
@@ -183,7 +183,7 @@ def tile_mix_aux_fm_none_kernel(tc, w, dy, v, e, out):
         for m in (0, 2):
             drain(on_scalar, m, 0)
             drain(on_scalar, m + 1, 0)
-            store(m, m + 2, 0, CHUNK)
+            store(m, m + 2, 0, CHUNK, nc.scalar if m else nc.sync)
 
         late = [(0, EARLY, HALF), (1, EARLY, HALF), (0, mid, HALF), (1, mid, HALF), (2, EARLY, CHUNK), (3, EARLY, CHUNK)]
 

from contextlib import ExitStack

import concourse.mybir as mybir

K, L, M, T = 1024, 1024, 512, 1536
FLOPS = 2 * (K + L) * M * T

F32 = mybir.dt.float32
BF16 = mybir.dt.bfloat16
U32 = mybir.dt.uint32
U8 = mybir.dt.uint8
E4M3 = mybir.dt.float8_e4m3fn_x4
E5M2 = mybir.dt.float8_e5m2_x4

P = 128
J = 4
K_PASS = P * J
CHUNK = 512
HALF = 256
EARLY = 1024
DMA_ALIGN = 256


def tile_mix_aux_fm_none_kernel(tc, w, dy, v, e, out):
    nc = tc.nc
    hbm = {"w": w, "dy": dy, "v": v, "e": e}
    fmt = {"w": E4M3, "dy": E5M2, "v": E4M3, "e": E4M3}
    on_vector, on_scalar = nc.vector.tensor_copy, nc.scalar.copy

    with ExitStack() as ctx:
        keep = ctx.enter_context(tc.tile_pool(name="keep", bufs=1))
        psum = ctx.enter_context(tc.psum_pool(name="psum", bufs=1))
        ctx.enter_context(tc.manual_schedule())

        width = {name: hbm[name].shape[1] for name in hbm}
        codes = {name: keep.tile([P, 2 * width[name]], U32, name="codes_" + name, align_bytes=64) for name in hbm}
        scales = {name: keep.tile([P, 2 * width[name]], U8, name="scales_" + name, align_bytes=64) for name in hbm}

        raw, staged = {}, {}

        def load(name, g, first, end):
            t = keep.tile([P, J, end - first], F32, name="raw_%s%d_%d" % (name, g, first), align_bytes=DMA_ALIGN)
            rows = hbm[name][g * K_PASS : (g + 1) * K_PASS, first:end]
            nc.sync.dma_start(out=t[:], in_=rows.rearrange("(p j) c -> p j c", j=J))
            for c in range(first, end, 64):
                raw[name, g, c] = t, first

        def load_both(name):
            t = keep.tile([P, 2, J * width[name]], F32, name="raw_" + name, align_bytes=DMA_ALIGN)
            nc.sync.dma_start(out=t[:], in_=hbm[name][:, :].rearrange("(g p j) c -> p g (j c)", g=2, j=J))
            raw[name] = t
            for g in range(2):
                for c in range(0, width[name], 64):
                    raw[name, g, c] = t[:, g, :].rearrange("p (j c) -> p j c", j=J), 0

        def stage(name, first, end):
            t = keep.tile([P, J * (end - first)], BF16, name="staged_%s%d" % (name, first), align_bytes=64)
            for word in range(first, end, 64):
                staged[name, word] = t, first

        def interleave(copy, name, g, first, end):
            src, src0 = raw[name, g, first]
            word = g * width[name] + first
            dst, dst0 = staged[name, word]
            lo = J * (word - dst0)
            copy(
                out=dst[:, lo : lo + J * (end - first)].rearrange("p (c i j) -> p c j i", i=4, j=J),
                in_=src[:, :, first - src0 : end - src0].rearrange("p j (c i) -> p c j i", i=4),
            )

        def interleave_both(copy, name):
            copy(
                out=staged[name, 0][0][:].rearrange("p (g c i j) -> p g c j i", g=2, i=4, j=J),
                in_=raw[name][:].rearrange("p g (j c i) -> p g c j i", j=J, i=4),
            )

        def quantise(name, first, end):
            src, src0 = staged[name, first]
            nc.vector.quantize_mx(
                out=codes[name][:, first:end].bitcast(fmt[name]),
                scales=scales[name][:, first:end],
                in_=src[:, J * (first - src0) : J * (end - src0)],
            )

        acc, done, total = {}, {}, {}

        def open_sum(m, t0, bank, n=CHUNK, passes=4):
            acc[m, t0] = psum.tile([P, CHUNK], F32, name="bank%d" % bank)[:, 0:n]
            done[m, t0], total[m, t0] = 0, passes

        def mm(m, t0, sta, mov, g, lo=0, hi=None):
            hi = hi or acc[m, t0].shape[1]
            rows = slice(g * M + m * P, g * M + (m + 1) * P)
            cols = slice(g * T + t0 + lo, g * T + t0 + hi)
            nc.tensor.matmul_mx(
                out=acc[m, t0][:, lo:hi],
                lhsT=codes[sta][:, rows].bitcast(fmt[sta]),
                lhsT_scale=scales[sta][:, rows],
                rhs=codes[mov][:, cols].bitcast(fmt[mov]),
                rhs_scale=scales[mov][:, cols],
                start=done[m, t0] == 0,
                stop=done[m, t0] == total[m, t0] - 1,
            )
            done[m, t0] += 1

        def drain(copy, m, t0, lo=0, hi=None):
            hi = hi or acc[m, t0].shape[1]
            copy(out=res[:, m, t0 + lo : t0 + hi], in_=acc[m, t0][:, lo:hi])

        def store(m0, m1, t0, t1, queue=nc.sync):
            rows = out[m0 * P : m1 * P, t0:t1]
            queue.dma_start(out=rows.rearrange("(m p) t -> p m t", p=P), in_=res[:, m0:m1, t0:t1])

        load("dy", 0, 0, T)
        load("dy", 1, 0, T)
        load_both("w")
        load("e", 0, 0, EARLY)
        load_both("v")
        load("e", 1, 0, CHUNK)
        load("e", 1, CHUNK, EARLY)
        load("e", 0, EARLY, T)
        load("e", 1, EARLY, T)

        tiles = range(M // P)
        early = [(m, t0) for t0 in (0, CHUNK) for m in tiles]
        mid = EARLY + HALF

        stage("dy", 0, T + CHUNK)
        stage("dy", T + CHUNK, 2 * T)
        interleave(on_scalar, "dy", 0, 0, T)
        res = keep.tile([P, M // P, T], F32, name="raw_dy0_0", align_bytes=DMA_ALIGN)
        interleave(on_scalar, "dy", 1, 0, CHUNK)
        interleave(on_vector, "dy", 1, CHUNK, T)
        quantise("dy", 0, EARLY)
        quantise("dy", T + CHUNK, 2 * T)
        quantise("dy", EARLY, T + CHUNK)
        stage("w", 0, M)
        stage("w", M, 2 * M)
        interleave(on_vector, "w", 0, 0, M)
        interleave(on_scalar, "w", 1, 0, M)
        quantise("w", M, 2 * M)
        quantise("w", 0, M)
        for bank, (m, t0) in enumerate(early):
            open_sum(m, t0, bank)
            mm(m, t0, "w", "dy", 0)
            mm(m, t0, "w", "dy", 1)

        stage("e", 0, CHUNK)
        stage("e", CHUNK, EARLY)
        interleave(on_vector, "e", 0, 0, CHUNK)
        interleave(on_scalar, "e", 0, CHUNK, EARLY)
        quantise("e", 0, CHUNK)
        quantise("e", CHUNK, EARLY)

        stage("v", 0, P)
        stage("v", P, M)
        stage("v", M, M + HALF)
        stage("v", M + HALF, 2 * M)
        interleave(on_scalar, "v", 0, 0, P)
        interleave(on_vector, "v", 0, P, M)
        interleave(on_scalar, "v", 1, HALF, M)
        quantise("v", 0, P)
        interleave(on_vector, "v", 1, 0, HALF)
        quantise("v", P, M)
        for m in tiles:
            for t0 in (0, CHUNK):
                mm(m, t0, "v", "e", 0)

        for c in range(0, EARLY, HALF):
            stage("e", T + c, T + c + HALF)
        interleave(on_scalar, "e", 1, HALF, CHUNK)
        quantise("v", M, M + HALF)
        interleave(on_vector, "e", 1, 0, HALF)
        quantise("v", M + HALF, 2 * M)
        quantise("e", T, T + HALF)
        quantise("e", T + HALF, T + CHUNK)
        for m in tiles:
            mm(m, 0, "v", "e", 1)
        for c in (CHUNK, CHUNK + HALF):
            interleave(on_vector, "e", 1, c, c + HALF)
        for c in (CHUNK, CHUNK + HALF):
            quantise("e", T + c, T + c + HALF)
        for m in (0, 2):
            drain(on_scalar, m, 0)
            drain(on_scalar, m + 1, 0)
            store(m, m + 2, 0, CHUNK, nc.scalar if m else nc.sync)

        late = [(0, EARLY, HALF), (1, EARLY, HALF), (0, mid, HALF), (1, mid, HALF), (2, EARLY, CHUNK), (3, EARLY, CHUNK)]

        def open_late(i):
            m, t0, n = late[i]
            open_sum(m, t0, i, n)
            mm(m, t0, "w", "dy", 0)
            mm(m, t0, "w", "dy", 1)

        def late_pass(g, first, end):
            for m, t0, n in late[first:end]:
                mm(m, t0, "v", "e", g)

        for i in range(2):
            open_late(i)
        for m in tiles:
            mm(m, CHUNK, "v", "e", 1)

        stage("e", EARLY, mid)
        stage("e", mid, T)
        for c in range(EARLY, mid, P):
            stage("e", T + c, T + c + P)
        for c in range(mid, T, P):
            stage("e", T + c, T + c + P)
        for c in (EARLY, mid):
            interleave(on_vector, "e", 0, c, c + HALF)
        for m in tiles[0:3]:
            drain(on_scalar, m, CHUNK)
        drain(on_vector, 3, CHUNK)
        store(0, 4, CHUNK, EARLY)
        for c in (EARLY, mid):
            quantise("e", c, c + HALF)
        for i in range(2, 6):
            open_late(i)
        late_pass(0, 0, 6)
        for c in (EARLY, mid):
            interleave(on_scalar, "e", 1, c, c + P)
            interleave(on_vector, "e", 1, c + P, c + HALF)
        for c in (EARLY, EARLY + P, mid + P, mid):
            quantise("e", T + c, T + c + P)
        late_pass(1, 0, 6)

        for t0 in (EARLY, mid):
            drain(on_scalar, 0, t0)
            drain(on_vector, 1, t0)
            store(0, 2, t0, t0 + HALF)
        drain(on_scalar, 2, EARLY)
        drain(on_vector, 3, EARLY)
        store(2, 4, EARLY, T)
